import numpy as np, ml_dtypes
CORES = [3,11,19,27,35,43,51,59]
N = 8
BF = ml_dtypes.bfloat16
def gentries(a):
    return np.ascontiguousarray(a.reshape(8, 16, -1).transpose(0, 2, 1)).reshape(8, -1)
def gtable(e):
    e = np.asarray(e); return np.ascontiguousarray(e.reshape(8, -1, 16).transpose(0, 2, 1)).reshape(128, -1).astype(np.int32)
F, A, GI, D, E, RO = 3072, 1536, 3, 1024, 192, 3
L = GI + RO - 1
R = 16 // N
NE = [F] + [A] * GI + [D] * (RO - 1)
ST = [sum(NE[:e]) + e * E for e in range(L + 1)]
PO = [0] + [sum(NE[1:e]) for e in range(1, L + 1)]
W = ST[L] + NE[L]; M = GI * A + (RO - 1) * D
def cols(e):
    o = np.concatenate([np.arange(ST[k], ST[k] + NE[k]) for k in range(e)]); g = np.concatenate([np.arange(ST[k] + NE[k], ST[k] + NE[k] + E) for k in range(e)])
    return o, g
def parts(rng):
    h = rng.integers(0, 65536, (N, 8, 16, F)); t = rng.integers(0, 65536, (8, 16))
    s = np.zeros((N, 8, GI * A), np.int64); d = np.zeros((N, 8, M), np.int64); m = np.zeros((N, 8, L * E), np.int64)
    for e in range(1, L + 1):
        o, g = cols(e); p, n = PO[e], NE[e]
        if e <= GI: s[:, :, p:p + n] = rng.choice(o, (N, 8, n))
        d[:, :, p:p + n] = np.where(rng.random((N, 8, n)) < 0.25, rng.choice(g, (N, 8, n)), rng.choice(o, (N, 8, n)))
    for e in range(L): m[:, :, e * E:(e + 1) * E] = rng.integers(0, NE[e], (N, 8, E))
    return h, t, s, d, m
def pack(h, t, s, d, m):
    return {"trait": np.ascontiguousarray(h.reshape(N, 128, F)).astype(np.int32), "aim0": np.tile(t.reshape(1, 128, 1), (N, 1, 1)).astype(np.int32),
            "sire": np.stack([gtable(a) for a in s]), "dam": np.stack([gtable(a) for a in d]), "mg": np.stack([gtable(a) for a in m])}
def setup_inputs(rng):
    return pack(*parts(rng))
def plant(rng, h, t, s, d, m, g, j, up):
    t[g] = rng.integers(0, 1000, 16); low = rng.integers(1000, 5000, 14)
    for q in range(N):
        c = 1 + rng.permutation(F - 1); x, y, z, a0, a1, b = [int(v) for v in c[:6]]; rest = c[6:]
        w = rng.integers(20000, 55000, (16, F)); w[0] = rng.integers(60000, 65536, F); w[1] = rng.integers(2000, 40000, F)
        w[:2, [x, y, z, b]] = rng.integers(2000, 40000, (2, 4)); w[1, b] = rng.integers(60000, 65536); w[0, x] = 1000; w[1, y] = 1000
        w[2:, y] = rng.integers(1000, 5000, 14) + 5000 * (q % 2); w[2:, x] = w[2:, y] + 40000; w[2:, z] = rng.integers(60000, 65536, 14)
        w[2:, a0] = low; w[2:, a1] = low + up; w[2:, b] = low + 40000; h[q, g] = w
        col = a1
        for e in range(1, GI):
            k = int(rng.integers(0, A)); s[q, g, PO[e] + k] = a0; d[q, g, PO[e] + k] = col; col = ST[e] + k
        o = rng.choice(rest, A); k = rng.permutation(A)[:4]; o[k[:3]] = (x, y, z); p = PO[GI]
        s[q, g, p:p + A] = o; d[q, g, p:p + A] = o; s[q, g, p + k[3]] = a0; d[q, g, p + k[3]] = col
        v = rng.choice(rest, D); v[int(rng.integers(1, D - 1))] = ST[GI] + k[3]; v[j] = b
        d[q, g, PO[GI + 1]:PO[GI + 1] + D] = v; m[q, g, (GI + 1) * E] = j
def setup_inputs_ends(rng):
    h, t, s, d, m = parts(rng); t = rng.choice(np.array([0, 1, 32767, 65534, 65535]), (8, 16))
    for e in range(1, L + 1):
        o, g = cols(e); p, n = PO[e], NE[e]
        if e <= GI: s[:, 4:, p:p + n] = rng.choice(np.array([0, F - 1, o[-1]]), (N, 4, n))
        d[:, 4:, p:p + n] = rng.choice(np.array([0, F - 1, F, F + E - 1, o[-1], g[-1]]), (N, 4, n))
    for e in range(L): m[:, 4:, e * E:(e + 1) * E] = rng.choice(np.array([0, NE[e] - 1]), (N, 4, E))
    h[:, :4, :, 7] = t[:4]; h[:, :4, :, 9] = np.where(t[:4] < 32768, 65535, 0); a, z = (GI - 1) * A, GI * A - 1
    for g in range(4):
        x, y = (7, 9) if g < 2 else (9, 7)
        s[:, g, z] = x; d[:, g, z] = x; s[:, g, a] = y; d[:, g, a] = y
    plant(rng, h, t, s, d, m, 6, D - 1, 1); plant(rng, h, t, s, d, m, 7, 0, 0)
    return pack(h, t, s, d, m)
def setup_inputs_ghosts(rng):
    h, t, s, d, m = parts(rng)
    for e in range(1, L + 1):
        o, g = cols(e); p, n = PO[e], NE[e]
        d[:, 0::2, p:p + n] = rng.choice(g, (N, 4, n)); d[:, 1, p:p + n] = rng.choice(o, (N, n))
        d[:, 6, p:p + n] = rng.integers(ST[e] - E, ST[e], (N, n))
        if e > GI: d[:, 3, p:p + n] = rng.integers(ST[e - 1], ST[e - 1] + NE[e - 1], (N, n))
    d[:, 3, :GI * A] = s[:, 3]
    for e in range(L):
        m[:, 5, e * E:(e + 1) * E] = rng.integers(0, NE[e], (N, 1)); m[:, 7, e * E:(e + 1) * E] = NE[e] - 1
    return pack(h, t, s, d, m)
def setup_inputs_lines(rng):
    h, t, s, d, m = parts(rng); t[5] = rng.integers(0, 65536)
    for e in range(1, L + 1):
        p, n = PO[e], NE[e]; lo, hi = ST[e - 1], ST[e - 1] + NE[e - 1]
        if e <= GI:
            s[:, 0:2, p:p + n] = rng.integers(lo, hi, (N, 2, n)); s[:, 2:4, p:p + n] = rng.integers(0, F, (N, 2, n))
            s[:, 4, p:p + n] = np.where(rng.random((N, n)) < 0.9, rng.integers(lo, hi, (N, 1)), rng.integers(lo, hi, (N, n)))
            d[:, 7, p:p + n] = rng.integers(1, ST[e], (N, 1))
        d[:, 0::4, p:p + n] = rng.integers(lo, hi, (N, 2, n)); d[:, 1::4, p:p + n] = rng.integers(0, F, (N, 2, n))
        for g, k in ((2, 1), (3, 2), (6, 3)):
            y = min(k, e - 1); d[:, g, p:p + n] = rng.integers(ST[y], ST[y] + NE[y], (N, n))
    return pack(h, t, s, d, m)
def setup_inputs_spread(rng):
    h, t, s, d, m = parts(rng)
    h = np.minimum((np.exp2(17 * rng.random((N, 8, 1, F))) * rng.random((N, 8, 16, F))).astype(np.int64), 65535)
    t = np.minimum(np.exp2(16 * rng.random((8, 16))).astype(np.int64), 65535)
    for e in range(1, L + 1):
        o, g = cols(e); p, n = PO[e], NE[e]; o = rng.permutation(o); g = rng.permutation(g)
        if e <= GI: s[:, :, p:p + n] = o[(len(o) * rng.random((N, 8, n)) ** 4).astype(np.int64)]
        d[:, :, p:p + n] = np.where(rng.random((N, 8, n)) < 0.5, g[(len(g) * rng.random((N, 8, n)) ** 3).astype(np.int64)], o[(len(o) * rng.random((N, 8, n)) ** 3).astype(np.int64)])
    for e in range(L): m[:, :, e * E:(e + 1) * E] = (NE[e] * rng.random((N, 8, E)) ** 3).astype(np.int64)
    return pack(h, t, s, d, m)
def setup_inputs_ties(rng):
    h, t, s, d, m = parts(rng)
    h[:, 0] = 5; t[0] = rng.choice(np.array([3, 4, 1000, 60000]), 16)
    t[0, 14] = 5; h[:, 0, 14, 0] = 60000; t[0, 15] = 0; h[:, 0, 15] = 65535
    s[:, 0] = np.where(s[:, 0] == 0, 1, s[:, 0]); d[:, 0] = np.where(d[:, 0] == 0, 1, d[:, 0]); m[:, 0, :E] = np.where(m[:, 0, :E] == 0, 1, m[:, 0, :E])
    h[:, 1:3] = rng.choice(np.array([0, 1, 32768, 65535]), (N, 2, 16, F)); t[1:3] = rng.choice(np.array([0, 1, 32768, 65535]), (2, 16))
    h[:, 3:5, 8:] = h[:, 3:5, :8]; t[3:5, 8:] = t[3:5, :8]
    h[:, 5] = 65535 * rng.integers(0, 2, (N, 16, F)); t[5] = 65535 * rng.integers(0, 2, 16)
    h[:, 6] = h[:, 6][:, :, np.arange(F) % 16]
    t[7] = 32768; h[:, 7] = 32768 + 20000 * (2 * rng.integers(0, 2, (N, 16, F)) - 1)
    return pack(h, t, s, d, m)
def check_inputs(d):
    bad = []
    for k in ("trait", "aim0"):
        if np.min(d[k]) < 0 or np.max(d[k]) > 65535: bad.append("range of " + k)
    if np.any(d["aim0"] != d["aim0"][:1]): bad.append("aim0 alike on all ranks")
    s = np.stack([gentries(a) for a in d["sire"]]); w = np.stack([gentries(a) for a in d["dam"]]); m = np.stack([gentries(a) for a in d["mg"]])
    for e in range(1, GI + 1):
        if not np.all(np.isin(s[:, :, PO[e]:PO[e] + NE[e]], cols(e)[0])): bad.append("sires of generation " + str(e))
    for e in range(1, L + 1):
        x = w[:, :, PO[e]:PO[e] + NE[e]]
        if np.min(x) < 0 or np.max(x) >= ST[e]: bad.append("dams of generation " + str(e))
    for e in range(L):
        x = m[:, :, e * E:(e + 1) * E]
        if np.min(x) < 0 or np.max(x) >= NE[e]: bad.append("emigrants of generation " + str(e))
    return bad
def pick(w, ix):
    return np.take_along_axis(w, ix[:, :, None, :], 3)
def reference(trait, aim0, sire, dam, mg):
    h = trait.astype(np.int64).reshape(N, 8, 16, F); t = aim0.astype(np.int64).reshape(N, 8, 16, 1)
    sl = np.zeros((N, 8, M), np.int64); sl[:, :, :GI * A] = np.stack([gentries(a) for a in sire])
    dl = np.stack([gentries(a) for a in dam]).astype(np.int64); ml = np.stack([gentries(a) for a in mg]).astype(np.int64)
    top = np.zeros((N, 8, W), np.int64); top[:, :, :F] = np.arange(F)
    for e in range(1, GI + 1): top[:, :, ST[e]:ST[e] + NE[e]] = np.take_along_axis(top, sl[:, :, PO[e]:PO[e] + NE[e]], 2)
    f = np.zeros((N, 8, 16, W)); aims = []
    for rnd in range(1, RO + 1):
        new = GI + rnd - 1
        for e in range(new + 1):
            a, n, p = ST[e], NE[e], PO[e]
            if e == 0: f[:, :, :, :F] = 65535 - np.abs(h - t)
            else: f[:, :, :, a:a + n] = (pick(f, sl[:, :, p:p + n]) + pick(f, dl[:, :, p:p + n])) * 0.5
            if e < L: f[:, :, :, a + n:a + n + E] = np.roll(pick(f[:, :, :, a:a + n], ml[:, :, e * E:(e + 1) * E]), 1, axis=0)
        if rnd == RO: break
        a, n = ST[new], NE[new]; x = f[:, :, :, a:a + n]
        best = a + np.argmax(x, axis=3); least = a + np.argmin(x, axis=3)
        b, p = ST[new + 1], PO[new + 1]
        row = np.argmin(pick(f, dl[:, :, p:p + D]), axis=2)
        sl[:, :, p:p + D] = np.take_along_axis(best, row, 2)
        old = np.take_along_axis(h, np.take_along_axis(top, least, 2)[:, :, :, None], 3)[:, :, :, 0]
        top[:, :, b:b + D] = np.take_along_axis(top, sl[:, :, p:p + D], 2)
        t1 = np.stack([old[m // R, :, m] for m in range(16)], axis=1)
        t = np.tile(t1.reshape(1, 8, 16, 1), (N, 1, 1, 1)); aims.append(t.reshape(N, 128))
    made = np.concatenate([f[:, :, :, ST[e]:ST[e] + NE[e]] for e in range(GI + 1, L + 1)], axis=3)
    return {"yf": made.reshape(N, 128, (RO - 1) * D).astype(np.float32), "ys": np.stack([gtable(a) for a in sl[:, :, GI * A:]]).astype(np.float32), "yt": np.stack(aims, axis=2).astype(np.float32)}

@@ -1,0 +1,494 @@
+from concourse.bass import DstId, RemoteDMATransfer
+from concourse.mybir import AluOpType as Op, ActivationFunctionType as Fn
+
+F, A, D, E = 3072, 1536, 1024, 192
+ST = [0, 3264, 4992, 6720, 8448, 9664]
+NV = 1536
+
+f32, i32, u16, bf = "float32", "int32", "uint16", "bfloat16"
+
+
+def _sb(n, t=f32):
+    return ("sbuf", [128, n], t)
+
+
+SCRATCH = {
+    "TI": _sb(3264, i32), "SI": _sb(288, i32), "DI": _sb(416, i32), "MI": _sb(64, i32), "AI": _sb(4, i32),
+    "SU": _sb(288, u16), "DU": _sb(416, u16), "MU": _sb(16, u16), "HU": _sb(48, u16), "LU": _sb(48, u16),
+    "CL": _sb(96, u16), "HI": _sb(48, i32), "HJ": _sb(48, i32), "LI": _sb(48, i32), "BASE": _sb(48, i32),
+    "PI": _sb(4, i32), "PJ": _sb(4, i32), "PF": _sb(4), "AR": _sb(16), "I16": _sb(16), "DM": _sb(16), "CC": _sb(8),
+    "WB": _sb(144), "WD": _sb(144), "ID": _sb(128), "EF": _sb(128), "EB": _sb(128, bf), "SEG": _sb(512),
+    "UF": _sb(16), "UO": _sb(16, u16), "IO": _sb(1536), "TC": _sb(4), "TH": _sb(4),
+    "X": _sb(6528), "X3": _sb(1536), "MD": _sb(1920), "X2": _sb(NV), "TA": _sb(9664), "TB": _sb(9664), "AB": _sb(1536),
+    "R1": _sb(1536), "R2": _sb(1536), "RS": _sb(1032), "K": _sb(1024), "Z": _sb(1344), "MK": _sb(768),
+    "PG": _sb(1024), "PH": _sb(1024), "JK": _sb(1536),
+    "SE0": _sb(192, i32), "SE1": _sb(384), "SE": _sb(192 * 8), "PE": _sb(192), "QE": _sb(192),
+    "AL": _sb(64), "G16": _sb(32), "CN": _sb(16), "IU": _sb(8, u16), "T16": _sb(64), "P16": _sb(48),
+    "UI": _sb(144, i32), "UJ": _sb(144, i32), "UB": _sb(144, bf), "MM": _sb(128, u16), "ZM": _sb(192), "CM": _sb(16, u16),
+    "YF": _sb(2048), "YS": _sb(128),
+    "HR": ("psum", [128, 2048], f32), "PT": ("psum", [128, 2048], f32),
+}
+PSUM = ("HR", "PT")
+PART = {"PM": 1024, "PN": 1536}
+SEMAPHORES = (["qv", "qs", "qp", "qg", "sent", "stored"] + ["ld%d" % k for k in range(10)]
+              + ["ar%d" % k for k in range(11)] + ["aim0s", "aim1s"])
+
+LOAD = [896, 896, 768, 512]
+GEN = [256, 448, 448, 384]
+GEN_VA = 256
+GEN_VH = 288
+NEW = [256, 448, 448, 384]
+P1 = [640, 896, 512, 128, 640]
+PV = 256
+G4 = [384, 384, 256]
+G5 = [512, 512]
+
+
+def _cuts(plan):
+    out, a = [], 0
+    for n in plan:
+        out.append((a, a + n))
+        a += n
+    return out
+
+
+def rank_program(g, core, T, topo):
+    q = T.rank_of(core)
+    if q is None:
+        return
+    N = len(T.cores)
+    nxt = T.cores[(q + 1) % N]
+    others = [T.cores[(q + k) % N] for k in range(1, N)]
+    queue = {"v": g.vector, "s": g.scalar, "p": g.tensor, "g": g, "y": g.sync}
+    count = {}
+    know = {k: {} for k in queue}
+    clock = {}
+    log = []
+
+    def c(name, a, b, s=None):
+        if name in PART:
+            name, a, b = "PT", a + PART[name], b + PART[name]
+        ap = T[name][:, a:b] if s is None else T[name][:, a:b:s]
+        if name in PSUM:
+            a, b = a // 512 * 512, -(-b // 512) * 512
+        return (ap, [(name, a, b)])
+
+    def ind(win, off):
+        return (win[0].indirect(off[0]), win[1] + off[1])
+
+    def val(x):
+        return x[0] if isinstance(x, tuple) else x
+
+    def regs(xs):
+        return [r for x in xs if isinstance(x, tuple) for r in x[1]]
+
+    def wait(e, sem, v):
+        if know[e].get(sem, 0) >= v:
+            return
+        queue[e].wait_ge(T.sem[sem], v)
+        know[e][sem] = v
+        for s, w in clock.get((sem, v), {}).items():
+            if know[e].get(s, 0) < w:
+                know[e][s] = w
+
+    def issue(e, fn, outs, ins, sem=None, inc=1):
+        wr, rd = regs(outs), regs(ins)
+        need = {}
+        for (name, lo, hi, w, eq, s, v) in log:
+            for (rs, mine) in ((wr, True), (rd, False)):
+                for (n2, a, b) in rs:
+                    if n2 == name and a < hi and lo < b and (w or mine or (name in PSUM and eq != e)):
+                        need[s] = max(need.get(s, 0), v)
+        for s in sorted(need, key=lambda s: -len(clock.get((s, need[s]), {}))):
+            wait(e, s, need[s])
+        sem = sem or "q" + e
+        count[sem] = count.get(sem, 0) + inc
+        ins_ = fn()
+        if ins_ is not None:
+            ins_.then_inc(T.sem[sem], inc)
+        clock[(sem, count[sem])] = dict(know[e])
+        for (rs, mine) in ((wr, True), (rd, False)):
+            for (n2, a, b) in rs:
+                log.append((n2, a, b, mine, e, sem, count[sem]))
+
+    def arrive(sem, v, outs):
+        count[sem] = v
+        for (n2, a, b) in regs(outs):
+            log.append((n2, a, b, True, "r", sem, v))
+
+    def copy(out, in_):
+        issue("v", lambda: g.vector.tensor_copy(out[0], in_[0]), [out], [in_])
+
+    def tt(out, a, b, op):
+        issue("v", lambda: g.vector.tensor_tensor(out[0], a[0], b[0], op), [out], [a, b])
+
+    def ts(out, a, s1, op0, s2=None, op1=None):
+        if op1 is None:
+            issue("v", lambda: g.vector.tensor_scalar(out[0], a[0], val(s1), None, op0), [out], [a, s1])
+        else:
+            issue("v", lambda: g.vector.tensor_scalar(out[0], a[0], val(s1), val(s2), op0, op1), [out], [a, s1, s2])
+
+    def scan(out, a, b, init, op0, op1):
+        issue("v", lambda: g.vector.tensor_tensor_scan(out[0], a[0], b[0], val(init), op0, op1), [out], [a, b, init])
+
+    def act(out, a, fn=Fn.Identity, bias=0.0, scale=1.0, acc=None):
+        if acc is None:
+            issue("s", lambda: g.scalar.activation(out[0], a[0], fn, bias=val(bias), scale=val(scale)), [out], [a, bias, scale])
+        else:
+            issue("s", lambda: g.scalar.activation(out[0], a[0], fn, bias=val(bias), scale=val(scale), accum_out=acc[0]),
+                  [out, acc], [a, bias, scale])
+
+    def iota(out, pat, base, mult, fl=False):
+        if fl:
+            issue("g", lambda: g.iota(out[0], pat, base, mult, allow_small_or_imprecise_dtypes=True), [out], [])
+        else:
+            issue("g", lambda: g.iota(out[0], pat, base, mult), [out], [])
+
+    def mm(out, pairs):
+        def fn():
+            for k, (l, r) in enumerate(pairs):
+                last = g.tensor.matmul(out[0], l[0], r[0], k == 0, k == len(pairs) - 1)
+            return last
+        issue("p", fn, [out], [x for p in pairs for x in p])
+
+    def fold16(out, w, src, lo, n):
+        mm(out, [(c(w, 15 - r, 143 - r), c(src, lo + r, lo + n, 16)) for r in range(16)])
+
+    nld = [0]
+
+    def load(e, out, src):
+        sem = "ld%d" % nld[0]
+        nld[0] += 1
+        issue(e, lambda: queue[e].dma_start(out[0], src), [out], [], sem, 16)
+
+    def store(dst, src):
+        issue("y", lambda: g.sync.dma_start(dst, src[0]), [], [src], "stored", 16)
+
+    nar = [0]
+    mask1 = topo.mask(core, nxt)
+    n1 = len(topo.engines(core, nxt))
+    nin = len(topo.engines(T.cores[(q - 1) % N], core))
+
+    def send(src, dst):
+        sem = "ar%d" % nar[0]
+        nar[0] += 1
+        rid, pid, _ = topo.addr(nxt)
+
+        def fn():
+            g.remote_dma(dst[0], src[0], T.sem[sem], T.sem.sent, pid, rid, mask1)
+        issue("g", fn, [], [src], "sent", n1)
+        arrive(sem, nin, [dst])
+
+    def common(a):
+        m = -1
+        for b in T.cores:
+            if b != a:
+                m &= topo.mask(a, b)
+        return m
+
+    def send_aims(r):
+        src = c("G16", 16 * r + 4 * (q // 2), 16 * r + 4 * (q // 2) + 4)
+        dst = c("AL", 32 * r + 4 * q, 32 * r + 4 * q + 4)
+        m = common(core)
+        sem = "aim%ds" % r
+
+        def fn():
+            ids = [DstId(rid=topo.addr(b)[0], pnc=topo.addr(b)[1]) for b in others]
+            g.remote_dma_fused([RemoteDMATransfer(dst_ids=ids, dma_engine_mask=m, remote_sem=T.sem[sem],
+                                                  srcs=[src[0]], dsts=[dst[0] for b in others])], local_sem=T.sem.sent)
+        issue("g", fn, [], [src], "sent", bin(m).count("1"))
+        copy(dst, src)
+        arrive(sem, sum(bin(common(b)).count("1") for b in others),
+               [c("AL", 32 * r + 4 * k, 32 * r + 4 * k + 4) for k in range(N) if k != q])
+
+    load("s", c("MI", 0, 60), T.mg[:])
+    load("s", c("AI", 0, 1), T.aim0[:])
+    lc = _cuts(LOAD)
+    load("y", c("SI", 0, 288), T.sire[:])
+    for a, b in lc:
+        load("y", c("TI", a, b), T.trait[:, a:b])
+    load("y", c("DI", 0, 416), T.dam[:])
+    iota(c("PI", 0, 1), [[0, 1]], 0, 1)
+    iota(c("AR", 0, 16), [[1, 16]], 0, 0, True)
+    iota(c("BASE", 0, 48), [[96, 4], [0, 12]], 0, 0)
+    iota(c("ID", 0, 128), [[-1, 128]], 0, 1, True)
+    iota(c("EF", 0, 128), [[-1, 2], [-2, 64]], 0, 1, True)
+    iota(c("UF", 0, 10), [[16, 10]], 23, 0, True)
+    iota(c("IO", 0, A), [[1, A]], 0, 0, True)
+    iota(c("X", F, F + E), [[0, E]], 0, 0, True)
+    iota(c("X", ST[2] - E, ST[2]), [[0, E]], 0, 0, True)
+    iota(c("RS", 0, 8), [[0, 8]], 0, 0, True)
+    issue("v", lambda: g.vector.memset(T.WB[:, 0:144], 0.0), [c("WB", 0, 144)], [])
+    ts(c("PJ", 0, 1), c("PI", 0, 1), 15, Op.bitwise_and)
+    ts(c("PJ", 1, 2), c("PI", 0, 1), 4, Op.arith_shift_right)
+    copy(c("PF", 0, 2), c("PJ", 0, 2))
+    pm, gk = c("PF", 0, 1), c("PF", 1, 2)
+    ts(c("I16", 0, 16), c("AR", 0, 16), pm, Op.is_equal)
+    ts(c("WB", 15, 144, 16), c("AR", 0, 9), gk, Op.is_equal)
+
+    ts(c("LI", 0, 48), c("MI", 12, 60), 15, Op.bitwise_and)
+    copy(c("LU", 0, 48), c("LI", 0, 48))
+    ts(c("HI", 0, 48), c("MI", 12, 60), 4, Op.arith_shift_right)
+    copy(c("MU", 0, 12), c("MI", 0, 12))
+    tt(c("HJ", 0, 48), c("HI", 0, 48), c("BASE", 0, 48), Op.add)
+    copy(c("HU", 0, 48), c("HJ", 0, 48))
+    act(c("MK", 0, 768), ind(c("I16", 0, 16), c("LU", 0, 48)))
+    own, nown = c("CC", 0, 1), c("CC", 1, 2)
+    act(own, c("I16", 2 * q, 2 * q + 1), Fn.Identity, c("I16", 2 * q + 1, 2 * q + 2))
+    act(c("CC", 4, 5), pm, Fn.Identity, -1024.0, 128.0)
+    act(c("JK", 0, 128), c("ID", 0, 128), Fn.Abs)
+    act(c("JK", 128, 256), c("EF", 0, 128), Fn.Abs)
+    act(nown, own, Fn.Identity, 1.0, -1.0)
+    act(c("DM", 0, 16), c("I16", 0, 16), Fn.Identity, 0.0, own)
+    act(c("ID", 0, 128), c("JK", 0, 128), Fn.Relu, 1.0, -1.0)
+    act(c("EB", 0, 128), c("JK", 128, 256), Fn.Relu, 1.0, -1.0)
+    act(c("WD", 0, 144), c("WB", 0, 144), Fn.Identity, 0.0, c("I16", (2 * q + 2) % 16, (2 * q + 2) % 16 + 1))
+    for r, eps in enumerate((128.0, 256.0)):
+        act(c("CC", 2 + r, 3 + r), pm, Fn.Identity, 15.0 / (8 * eps), -1.0 / (8 * eps))
+    t0, h0 = c("TC", 0, 1), c("TH", 0, 1)
+    copy(t0, c("AI", 0, 1))
+    ts(h0, t0, 0.5, Op.mult)
+
+    def founders(k):
+        a, b = lc[k]
+        copy(c("X", a, b), c("TI", a, b))
+        act(c("TA", a, b), c("X", a, b), Fn.Abs, t0, -1.0)
+
+    tt(c("Z", 0, 576), ind(c("SI", 0, 288), c("HU", 0, 36)), c("MK", 0, 576), Op.mult)
+    fold16(c("PM", 0, 36), "WB", "Z", 0, 576)
+    copy(c("SU", 0, 288), c("SI", 0, 288))
+    for k in range(len(lc) - 1):
+        founders(k)
+    copy(c("SE0", 0, E), ind(c("TI", 0, F), c("MU", 0, 12)))
+    send(c("SE0", 0, E), c("TI", F, F + E))
+    founders(len(lc) - 1)
+
+    s1, s2 = ST[1], ST[2]
+
+    def split(out, o, n, wv, ws, lst, l0):
+        copy(c(out, o, o + n), ind(wv, c(lst, l0, l0 + n // 16)))
+        act(c(out, o + n, o + A), ind(ws, c(lst, l0 + n // 16, l0 + 96)))
+
+    copy(c("CL", 0, 36), c("PM", 0, 36))
+    tt(c("Z", 576, 1344), ind(c("DI", 0, 416), c("HU", 0, 48)), c("MK", 0, 768), Op.mult)
+    fold16(c("PN", 0, 48), "WB", "Z", 576, 768)
+    split("X", s1, P1[0], c("TI", 0, F), c("X", 0, F), "SU", 0)
+    copy(c("SE1", 0, E), ind(c("TI", 0, F), c("CL", 0, 12)))
+    send(c("SE1", 0, E), c("MD", A + E, A + 2 * E))
+    iota(c("SEG", 0, 512), [[0, 32], [32767, 16]], 0, 0, True)
+    copy(c("DU", 0, 416), c("DI", 0, 416))
+    split("X", s2, P1[1], c("X", 0, s1 + A), c("X", 0, s1 + A), "SU", 96)
+    act(c("HR", 0, A), c("X", s1, s1 + A), Fn.Abs, h0, -0.5)
+    copy(c("CL", 36, 84), c("PN", 0, 48))
+
+    wi = c("TI", 0, s1)
+    copy(c("SE1", E, 2 * E), ind(wi, c("CL", 36, 48)))
+    send(c("SE1", E, 2 * E), c("MD", A, A + E))
+    copy(c("X", F, s1), c("TI", F, s1))
+    n, m = P1[2], (P1[2] + A) // 64 * 32
+    copy(c("MD", n, m), ind(wi, c("DU", n // 16, m // 16)))
+    act(c("MD", 0, n), ind(c("X", 0, s1), c("DU", 0, n // 16)))
+    copy(c("MD", m, A), ind(wi, c("DU", m // 16, 96)))
+    act(c("TA", s1, s1 + m), c("MD", 0, m), Fn.Abs, h0, -0.5)
+    act(c("TA", s1 + m, s1 + A), c("MD", m, A), Fn.Abs, h0, -0.5)
+    copy(c("X3", 0, P1[3]), ind(c("X", 0, s2 + A), c("SU", 192, 192 + P1[3] // 16)))
+    tt(c("TA", s1, s1 + m), c("TA", s1, s1 + m), c("HR", 0, m), Op.add)
+    act(c("TA", F, s1), c("X", F, s1), Fn.Abs, t0, -1.0)
+    tt(c("TA", s1 + m, s1 + A), c("TA", s1 + m, s1 + A), c("HR", m, A), Op.add)
+    act(c("HR", A, A + E), c("MD", A + E, A + 2 * E), Fn.Abs, h0, -0.5)
+    act(c("X3", P1[3], P1[4]), ind(c("X", 0, s2 + A), c("SU", 192 + P1[3] // 16, 192 + P1[4] // 16)))
+
+    def first_ghosts():
+        act(c("TA", s1 + A, s2), c("MD", A, A + E), Fn.Abs, h0, -0.5)
+        tt(c("TA", s1 + A, s2), c("TA", s1 + A, s2), c("HR", A, A + E), Op.add)
+
+    nse = [0]
+
+    def sendbuf():
+        nse[0] += 1
+        return c("SE", E * (nse[0] - 1), E * nse[0])
+
+    def least_tail(n, cut, r, win):
+        big = c("R1", n - 1, n)
+        act(c("JK", cut, n), c("R1", cut, n), Fn.Sign, big, -1.0, c("CN", 1, 2))
+        ts(c("CN", 2, 3), c("R1", cut - 1, cut), big, Op.is_lt, float(cut), Op.mult)
+        ts(c("IU", 0, 1), c("CN", 2, 3), c("CN", 0, 1), Op.max, c("CN", 1, 2), Op.add)
+        tt(c("G16", 16 * r, 16 * r + 16), ind(win, c("IU", 0, 1)), c("DM", 0, 16), Op.mult)
+        send_aims(r)
+
+    def least_step(tb, s, a, b, cut):
+        x = c(tb, s + a, s + b)
+        scan(c("R1", a, b), x, x, 0.0 if a == 0 else c("R1", a - 1, a), Op.max, Op.max)
+        if b == cut:
+            act(c("JK", 0, cut), c("R1", 0, cut), Fn.Sign, c("R1", cut - 1, cut), -1.0, c("CN", 0, 1))
+
+    def generation(tb, e, newest, pre=None):
+        s = ST[e]
+        ws, wd = c(tb, 0, s - E), c(tb, 0, s)
+        cuts = _cuts(NEW if newest else GEN)
+        o = (e - 1) * 96
+        sb = sendbuf()
+        sl, dl = c("CL", 12 * (e - 1), 12 * e), c("CL", 36 + 12 * (e - 1), 36 + 12 * e)
+        va = cuts[0][1] if newest else GEN_VA
+        act(c("PE", 0, E), ind(ws, sl))
+        copy(c("AB", 0, va), ind(ws, c("SU", o, o + va // 16)))
+        if pre:
+            pre()
+        if newest:
+            tt(sb, ind(wd, dl), c("PE", 0, E), Op.add)
+        else:
+            tt(c("QE", 0, E), ind(wd, dl), c("PE", 0, E), Op.add)
+            ts(sb, c("QE", 0, E), 0.5, Op.mult)
+        send(sb, c(tb, s + A, s + A + E))
+        for a, b in cuts:
+            if b > va:
+                a = max(a, va)
+                act(c("AB", a, b), ind(ws, c("SU", o + a // 16, o + b // 16)))
+        if newest:
+            act(c("X3", P1[4], A), ind(c("X", 0, s2 + A), c("SU", 192 + P1[4] // 16, 288)))
+        cut = cuts[-1][0]
+        for k, (a, b) in enumerate(cuts):
+            du = c("DU", o + a // 16, o + b // 16)
+            if newest:
+                tt(c(tb, s + a, s + b), ind(wd, du), c("AB", a, b), Op.add)
+                if b >= cut:
+                    least_step(tb, s, 0 if b == cut else a, b, cut)
+            else:
+                tt(c("AB", a, b), ind(wd, du), c("AB", a, b), Op.add)
+                h = min(b, A - GEN_VH)
+                act(c(tb, s + a, s + h), c("AB", a, h), Fn.Identity, 0.0, 0.5)
+                if h < b:
+                    ts(c(tb, s + h, s + b), c("AB", h, b), 0.5, Op.mult)
+        return cut
+
+    def sires_out(r):
+        act(c("YS", 64 * r, 64 * r + 64), c("PM", 0, 64), Fn.Identity, float(ST[3 + r]))
+
+    def choose(tb, r):
+        e = 3 + r
+        s, n = ST[e], (A if r == 0 else D)
+        eps = 128.0 if r == 0 else 256.0
+        x = c(tb, s, s + n)
+        ce = c("CC", 2 + r, 3 + r)
+        scan(c("R2", 0, n), x, x, 1.0e9, Op.min, Op.min)
+        o = 288 + 64 * r
+        act(c("K", 0, D), ind(c(tb, 0, ST[e + 1]), c("DU", o, o + 64)), Fn.Identity, ce, 0.125)
+        act(c("JK", 0, n), c("R2", 0, n), Fn.Sign, c("R2", n - 1, n), -1.0, c("CN", 4, 5))
+        if r == 0:
+            ts(c("CC", 5, 6), c("CC", 4, 5), 4.0, Op.mult, c("CC", 4, 5), Op.min)
+            ts(c("UO", 0, 10), c("UF", 0, 10), c("CC", 5, 6), Op.add, 1031.0, Op.min)
+            act(c("X", s2 - E, s2), c("MD", A + E, A + 2 * E))
+            act(c("X2", 0, NV), c("X", 0, NV), Fn.Identity, 0.0, 2.0)
+        else:
+            sires_out(0)
+        for h in range(2):
+            def fn():
+                for u in range(4 * h, 4 * h + 4):
+                    last = g.tensor.transpose(T.PT[:, 128 * u:128 * u + 128], T.K[:, u:D:8], T.ID[:, 0:128])
+                return last
+            issue("p", fn, [c("PT", 512 * h, 512 * h + 512)], [c("K", 0, D), c("ID", 0, 128)])
+        for h in range(2):
+            scan(c("RS", 8 + 512 * h, 520 + 512 * h), c("SEG", 0, 512), c("PT", 512 * h, 512 * h + 512), 0.0, Op.min, Op.max)
+        ts(c("UI", 0, 144), ind(c("RS", 0, 1032), c("UO", 0, 9)), 8 * eps, Op.mult)
+        bu = c("IU", 2 + 2 * r, 3 + 2 * r)
+        ts(bu, c("CN", 4, 5), -1.0, Op.mult)
+        ts(c("UJ", 0, 144), c("UI", 0, 144), 15, Op.bitwise_and)
+        copy(c("UB", 0, 144), c("UJ", 0, 144))
+        mm(c("PM", 0, 64), [(c("UB", 8, 136), c("EB", 0, 64)), (c("UB", 0, 128), c("EB", 64, 128))])
+        ml = c("MM", 64 * r, 64 * r + 64)
+        p16 = c("P16", 32, 48)
+        if r == 0:
+            ts(c("P16", 0, 16), ind(c("X3", 0, A), bu), own, Op.mult)
+            ts(c("P16", 16, 32), ind(c("IO", 0, A), bu), nown, Op.mult)
+            ts(c("DI", 288, 352), c("PM", 0, 64), -1.0, Op.mult, 15.0, Op.add)
+            tt(p16, c("P16", 0, 16), c("P16", 16, 32), Op.add)
+            copy(ml, c("DI", 288, 352))
+            tt(c("ZM", 0, E), ind(c("DI", 0, 352), c("HU", 36, 48)), c("MK", 576, 768), Op.mult)
+            fold16(c("PN", 0, 12), "WB", "ZM", 0, E)
+        else:
+            copy(p16, ind(c("IO", 0, A), bu))
+            ts(ml, c("PM", 0, 64), -1.0, Op.mult, 15.0, Op.add)
+
+    def payload(r, part):
+        pg, p16 = ("PG" if r == 0 else "PH"), c("P16", 32, 48)
+        if part == 0:
+            copy(c(pg, 0, PV), ind(p16, c("MM", 64 * r, 64 * r + PV // 16)))
+        else:
+            act(c(pg, PV, D), ind(p16, c("MM", 64 * r + PV // 16, 64 * r + 64)))
+            fold16(c("PM", 0, 64), "WD", pg, 0, D)
+
+    def start_round(tb, r):
+        t, h = c("TC", r, r + 1), c("TH", r, r + 1)
+        al = c("AL", 32 * (r - 1), 32 * r)
+        act(c("JK", 0, 32), al, Fn.Identity, 0.0, 1.0, t)
+        act(c("JK", 32, 64), al, Fn.Identity, 0.0, 0.5, h)
+        act(c(tb, s1, s2), c("MD", 0, A + E), Fn.Abs, h, -0.5)
+        act(c("HR", 0, A + E), c("X", s1, s2), Fn.Abs, h, -0.5)
+        act(c(tb, NV, s1), c("X", NV, s1), Fn.Abs, t, -1.0)
+        ts(c("PT", 0, NV), c("X2", 0, NV), t, Op.subtract, t, Op.max)
+        tt(c(tb, 0, NV), c("PT", 0, NV), c("X", 0, NV), Op.subtract)
+        if r == 1:
+            copy(c("CM", 0, 12), c("PN", 0, 12))
+        tt(c(tb, s1, s2), c(tb, s1, s2), c("HR", 0, A + E), Op.add)
+
+    def fourth(tb, r):
+        s = ST[4]
+        wd = c(tb, 0, s)
+        payload(r - 1, 0)
+        t16 = c("T16", 16 * r, 16 * r + 16)
+        ts(t16, ind(c(tb, ST[3], ST[3] + A), c("IU", 2, 3)), 0.5, Op.mult)
+        act(c("QE", 0, E), ind(wd, c("CL", 72, 84)), Fn.Identity, 0.0, 0.5)
+        sb = sendbuf()
+        cuts = _cuts(G4)
+        a, b = cuts[0]
+        h = (a + b) // 64 * 32
+        ts(c("AB", a, h), ind(wd, c("DU", 288 + a // 16, 288 + h // 16)), 0.5, Op.mult)
+        tt(sb, ind(t16, c("CM", 0, 12)), c("QE", 0, E), Op.add)
+        send(sb, c(tb, s + D, s + D + E))
+        cut = cuts[-1][0]
+        for k, (a, b) in enumerate(cuts):
+            lo = h if k == 0 else a
+            act(c("AB", lo, b), ind(wd, c("DU", 288 + lo // 16, 288 + b // 16)), Fn.Identity, 0.0, 0.5)
+        payload(r - 1, 1)
+        for k, (a, b) in enumerate(cuts):
+            tt(c(tb, s + a, s + b), ind(t16, c("MM", a // 16, b // 16)), c("AB", a, b), Op.add)
+            if r == 1 and b >= cut:
+                least_step(tb, s, 0 if b == cut else a, b, cut)
+        return cut
+
+    generation("TA", 2, False, first_ghosts)
+    cut = generation("TA", 3, True)
+    least_tail(A, cut, 0, c("X3", 0, A))
+    choose("TA", 0)
+    start_round("TB", 1)
+    generation("TB", 2, False)
+    generation("TB", 3, False)
+    cut = fourth("TB", 1)
+    least_tail(D, cut, 1, c("PG", 0, D))
+    choose("TB", 1)
+    start_round("TA", 2)
+    store(T.yt[:], c("TC", 1, 3))
+    generation("TA", 2, False)
+    generation("TA", 3, False)
+    fourth("TA", 2)
+    t16 = c("T16", 48, 64)
+    ts(t16, ind(c("TA", ST[4], ST[4] + D), c("IU", 4, 5)), -0.5, Op.mult)
+    act(c("YF", 0, 512), c("TA", ST[4], ST[4] + 512), Fn.Identity, 65535.0, -1.0)
+    ts(c("YF", 512, D), c("TA", ST[4] + 512, ST[4] + D), -1.0, Op.mult, 65535.0, Op.add)
+    store(T.yf[:, 0:D], c("YF", 0, D))
+    wd = c("TA", 0, ST[5])
+    cuts = _cuts(G5)
+    for k, (a, b) in enumerate(cuts):
+        if k == 0:
+            h = (a + b) // 64 * 32
+            ts(c("AB", a, h), ind(wd, c("DU", 352 + a // 16, 352 + h // 16)), -0.5, Op.mult, 65535.0, Op.add)
+            a = h
+        act(c("AB", a, b), ind(wd, c("DU", 352 + a // 16, 352 + b // 16)), Fn.Identity, 65535.0, -0.5)
+    sires_out(1)
+    for k, (a, b) in enumerate(cuts):
+        tt(c("YF", D + a, D + b), ind(t16, c("MM", 64 + a // 16, 64 + b // 16)), c("AB", a, b), Op.add)
+        store(T.yf[:, D + a:D + b], c("YF", D + a, D + b))
+        if k == 0:
+            store(T.ys[:], c("YS", 0, 128))
+    for sem in sorted(count):
+        wait("y" if sem == "stored" else "g", sem, count[sem])

@@ -1,9 +1,10 @@
 from concourse.bass import DstId, RemoteDMATransfer
-from concourse.mybir import AluOpType as Op, ActivationFunctionType as Fn
+from concourse.mybir import AluOpType as Op, ActivationFunctionType as Fn, AxisListType as Ax
 
 F, A, D, E = 3072, 1536, 1024, 192
 ST = [0, 3264, 4992, 6720, 8448, 9664]
-NV = 1536
+NV = 1024
+NP = 1024
 
 f32, i32, u16, bf = "float32", "int32", "uint16", "bfloat16"
 
@@ -13,35 +14,54 @@ def _sb(n, t=f32):
 
 
 SCRATCH = {
-    "TI": _sb(3264, i32), "SI": _sb(288, i32), "DI": _sb(416, i32), "MI": _sb(64, i32), "AI": _sb(4, i32),
+    "TI": _sb(3072, i32), "IO": _sb(1536, i32), "SI": _sb(288, i32), "DI": _sb(416, i32), "MI": _sb(64, i32), "AI": _sb(4, i32),
     "SU": _sb(288, u16), "DU": _sb(416, u16), "MU": _sb(16, u16), "HU": _sb(48, u16), "LU": _sb(48, u16),
     "CL": _sb(96, u16), "HI": _sb(48, i32), "HJ": _sb(48, i32), "LI": _sb(48, i32), "BASE": _sb(48, i32),
     "PI": _sb(4, i32), "PJ": _sb(4, i32), "PF": _sb(4), "AR": _sb(16), "I16": _sb(16), "DM": _sb(16), "CC": _sb(8),
-    "WB": _sb(144), "WD": _sb(144), "ID": _sb(128), "EF": _sb(128), "EB": _sb(128, bf), "SEG": _sb(512),
-    "UF": _sb(16), "UO": _sb(16, u16), "IO": _sb(1536), "TC": _sb(4), "TH": _sb(4),
-    "X": _sb(6528), "X3": _sb(1536), "MD": _sb(1920), "X2": _sb(NV), "TA": _sb(9664), "TB": _sb(9664), "AB": _sb(1536),
+    "WB": _sb(144), "WD": _sb(144), "ID": _sb(160), "EF": _sb(128), "EB": _sb(128), "UF": _sb(16), "UO": _sb(16, u16),
+    "SEG": _sb(512), "HP": _sb(128), "HN": _sb(128), "TC": _sb(4), "TH": _sb(4), "TV": _sb(4),
+    "X": _sb(6528), "X3": _sb(1536), "MD": _sb(1536), "X2": _sb(NV), "TA": _sb(9664), "TB": _sb(9664), "AB": _sb(1536),
     "R1": _sb(1536), "R2": _sb(1536), "RS": _sb(1032), "K": _sb(1024), "Z": _sb(1344), "MK": _sb(768),
-    "PG": _sb(1024), "PH": _sb(1024), "JK": _sb(1536),
-    "SE0": _sb(192, i32), "SE1": _sb(384), "SE": _sb(192 * 8), "PE": _sb(192), "QE": _sb(192),
-    "AL": _sb(64), "G16": _sb(32), "CN": _sb(16), "IU": _sb(8, u16), "T16": _sb(64), "P16": _sb(48),
-    "UI": _sb(144, i32), "UJ": _sb(144, i32), "UB": _sb(144, bf), "MM": _sb(128, u16), "ZM": _sb(192), "CM": _sb(16, u16),
+    "PG": _sb(1024), "PH": _sb(1024, bf), "JK": _sb(1536, bf), "J3": _sb(96), "J4": _sb(160),
+    "SE0": _sb(192, u16), "GU": _sb(192, u16), "SE1": _sb(384), "GP": _sb(384), "GT": _sb(384),
+    "SE": _sb(192 * 8), "PE": _sb(192), "QE": _sb(192),
+    "AL": _sb(96), "CN": _sb(16), "IU": _sb(16, u16), "T16": _sb(64), "P16": _sb(80),
+    "UJ": _sb(64, i32), "UB": _sb(144), "MM": _sb(128, u16), "ZM": _sb(192, bf), "WF": _sb(144, bf), "WH": _sb(144, bf),
+    "PB": _sb(16, bf), "CM": _sb(16, u16),
     "YF": _sb(2048), "YS": _sb(128),
     "HR": ("psum", [128, 2048], f32), "PT": ("psum", [128, 2048], f32),
 }
 PSUM = ("HR", "PT")
-PART = {"PM": 1024, "PN": 1536}
+PART = {"AV": ("HR", 0), "DL": ("PT", 0), "BA": ("HR", 1536), "BB": ("PT", 1536)}
 SEMAPHORES = (["qv", "qs", "qp", "qg", "sent", "stored"] + ["ld%d" % k for k in range(10)]
               + ["ar%d" % k for k in range(11)] + ["aim0s", "aim1s"])
 
 LOAD = [896, 896, 768, 512]
-GEN = [256, 448, 448, 384]
-GEN_VA = 256
-GEN_VH = 288
-NEW = [256, 448, 448, 384]
-P1 = [640, 896, 512, 128, 640]
-PV = 256
+GEN = [512, 576, 448]
+NEW = [448, 704, 384]
+P1 = [768, 512]
+X2V = 896
+X3P = [128, 640, 1536]
+PVR = [384, 256]
 G4 = [384, 384, 256]
-G5 = [512, 512]
+G4V = 192
+G5 = [256, 448, 320]
+G5V = 128
+KV = [384, 512]
+DAG = {}
+ORDER = [
+    0, 2, 1, 5, 3, 4, 6, 7, 8, 9, 13, 10, 15, 50, 48, 11, 49, 14, 12, 61, 62, 63, 60, 16, 17, 18, 35, 51, 19, 54, 20, 21, 23, 22, 24, 30, 25,
+    29, 39, 44, 38, 34, 37, 26, 52, 27, 36, 53, 31, 42, 28, 64, 40, 43, 46, 41, 65, 32, 57, 56, 33, 68, 70, 73, 83, 67, 79, 81, 58, 59, 69,
+    80, 75, 85, 86, 84, 82, 71, 72, 87, 88, 92, 91, 94, 93, 96, 99, 95, 74, 98, 102, 108, 76, 78, 89, 77, 90, 101, 109, 110, 111, 112, 115,
+    114, 119, 116, 117, 120, 118, 55, 121, 122, 97, 123, 100, 127, 128, 129, 45, 130, 113, 131, 124, 125, 132, 133, 134, 135, 136, 138, 137,
+    139, 140, 141, 126, 144, 142, 143, 103, 107, 105, 104, 145, 147, 66, 148, 149, 146, 154, 152, 106, 155, 150, 153, 166, 169, 170, 175,
+    168, 167, 151, 171, 158, 172, 178, 173, 177, 174, 176, 180, 181, 182, 186, 190, 185, 187, 188, 159, 156, 189, 191, 157, 192, 161, 193,
+    162, 194, 183, 184, 160, 195, 196, 197, 198, 199, 200, 201, 164, 202, 204, 165, 206, 163, 207, 179, 203, 47, 205, 209, 211, 210, 215,
+    216, 212, 213, 214, 219, 220, 221, 217, 218, 222, 223, 224, 225, 233, 226, 208, 227, 228, 232, 229, 230, 231, 234, 236, 237, 238, 250,
+    253, 254, 252, 259, 260, 235, 239, 251, 242, 255, 256, 257, 261, 258, 262, 264, 265, 266, 267, 268, 270, 269, 274, 271, 240, 272, 276,
+    241, 247, 277, 278, 275, 244, 273, 243, 280, 281, 282, 245, 285, 288, 286, 290, 287, 289, 291, 279, 292, 283, 284, 293, 295, 300, 294,
+    246, 296, 297, 248, 303, 301, 302, 249, 306, 309, 312, 313, 298, 299, 315, 304, 314, 310, 307, 316, 319, 321, 317, 322, 263, 305, 311,
+    308, 324, 318, 326, 320, 323, 325, 327]
 
 
 def _cuts(plan):
@@ -57,17 +77,18 @@ def rank_program(g, core, T, topo):
     if q is None:
         return
     N = len(T.cores)
-    nxt = T.cores[(q + 1) % N]
     others = [T.cores[(q + k) % N] for k in range(1, N)]
     queue = {"v": g.vector, "s": g.scalar, "p": g.tensor, "g": g, "y": g.sync}
     count = {}
     know = {k: {} for k in queue}
     clock = {}
-    log = []
+    log = {}
+    ops = []
+    DAG["ops"] = ops
 
     def c(name, a, b, s=None):
         if name in PART:
-            name, a, b = "PT", a + PART[name], b + PART[name]
+            name, a, b = PART[name][0], a + PART[name][1], b + PART[name][1]
         ap = T[name][:, a:b] if s is None else T[name][:, a:b:s]
         if name in PSUM:
             a, b = a // 512 * 512, -(-b // 512) * 512
@@ -93,28 +114,41 @@ def rank_program(g, core, T, topo):
 
     def issue(e, fn, outs, ins, sem=None, inc=1):
         wr, rd = regs(outs), regs(ins)
-        need = {}
-        for (name, lo, hi, w, eq, s, v) in log:
-            for (rs, mine) in ((wr, True), (rd, False)):
-                for (n2, a, b) in rs:
-                    if n2 == name and a < hi and lo < b and (w or mine or (name in PSUM and eq != e)):
-                        need[s] = max(need.get(s, 0), v)
-        for s in sorted(need, key=lambda s: -len(clock.get((s, need[s]), {}))):
-            wait(e, s, need[s])
-        sem = sem or "q" + e
-        count[sem] = count.get(sem, 0) + inc
-        ins_ = fn()
-        if ins_ is not None:
-            ins_.then_inc(T.sem[sem], inc)
-        clock[(sem, count[sem])] = dict(know[e])
+        deps = set()
         for (rs, mine) in ((wr, True), (rd, False)):
             for (n2, a, b) in rs:
-                log.append((n2, a, b, mine, e, sem, count[sem]))
+                for (lo, hi, w, eq, k) in log.get(n2, ()):
+                    if a < hi and lo < b and (w or mine or (n2 in PSUM and eq != e)):
+                        deps.add(k)
+        for (rs, mine) in ((wr, True), (rd, False)):
+            for (n2, a, b) in rs:
+                log.setdefault(n2, []).append((a, b, mine, e, len(ops)))
+        ops.append((e, fn, wr, rd, sem or "q" + e, inc, deps))
 
     def arrive(sem, v, outs):
-        count[sem] = v
         for (n2, a, b) in regs(outs):
-            log.append((n2, a, b, True, "r", sem, v))
+            log.setdefault(n2, []).append((a, b, True, "r", len(ops)))
+        ops.append(("r", None, regs(outs), [], sem, v, {len(ops) - 1}))
+
+    def emit():
+        order = ORDER if len(ORDER) == len(ops) else range(len(ops))
+        done = {}
+        for k in order:
+            e, fn, _, _, sem, inc, deps = ops[k]
+            count[sem] = count.get(sem, 0) + inc
+            if e != "r":
+                need = {}
+                for j in deps:
+                    need[done[j][0]] = max(need.get(done[j][0], 0), done[j][1])
+                for s in sorted(need, key=lambda s: -len(clock.get((s, need[s]), {}))):
+                    wait(e, s, need[s])
+                ins_ = fn()
+                if ins_ is not None:
+                    ins_.then_inc(T.sem[sem], inc)
+                clock[(sem, count[sem])] = dict(know[e])
+            done[k] = (sem, count[sem])
+        for sem in sorted(count):
+            wait("y" if sem == "stored" else "g", sem, count[sem])
 
     def copy(out, in_):
         issue("v", lambda: g.vector.tensor_copy(out[0], in_[0]), [out], [in_])
@@ -165,19 +199,17 @@ def rank_program(g, core, T, topo):
         issue("y", lambda: g.sync.dma_start(dst, src[0]), [], [src], "stored", 16)
 
     nar = [0]
-    mask1 = topo.mask(core, nxt)
-    n1 = len(topo.engines(core, nxt))
-    nin = len(topo.engines(T.cores[(q - 1) % N], core))
 
     def send(src, dst):
         sem = "ar%d" % nar[0]
         nar[0] += 1
-        rid, pid, _ = topo.addr(nxt)
+        to = T.cores[(q + 1) % N]
+        rid, pid, _ = topo.addr(to)
 
         def fn():
-            g.remote_dma(dst[0], src[0], T.sem[sem], T.sem.sent, pid, rid, mask1)
-        issue("g", fn, [], [src], "sent", n1)
-        arrive(sem, nin, [dst])
+            g.remote_dma(dst[0], src[0], T.sem[sem], T.sem.sent, pid, rid, topo.mask(core, to))
+        issue("g", fn, [], [src], "sent", len(topo.engines(core, to)))
+        arrive(sem, len(topo.engines(T.cores[(q - 1) % N], core)), [dst])
 
     def common(a):
         m = -1
@@ -187,38 +219,35 @@ def rank_program(g, core, T, topo):
         return m
 
     def send_aims(r):
-        src = c("G16", 16 * r + 4 * (q // 2), 16 * r + 4 * (q // 2) + 4)
-        dst = c("AL", 32 * r + 4 * q, 32 * r + 4 * q + 4)
+        o = 48 * r
+        src = c("AL", o + 4 * (q // 2), o + 4 * (q // 2) + 4)
+        slots = [c("AL", o + 12 + 4 * k, o + 16 + 4 * k) for k in range(1, N)]
         m = common(core)
         sem = "aim%ds" % r
 
         def fn():
             ids = [DstId(rid=topo.addr(b)[0], pnc=topo.addr(b)[1]) for b in others]
             g.remote_dma_fused([RemoteDMATransfer(dst_ids=ids, dma_engine_mask=m, remote_sem=T.sem[sem],
-                                                  srcs=[src[0]], dsts=[dst[0] for b in others])], local_sem=T.sem.sent)
+                                                  srcs=[src[0]], dsts=[s[0] for s in slots])], local_sem=T.sem.sent)
         issue("g", fn, [], [src], "sent", bin(m).count("1"))
-        copy(dst, src)
-        arrive(sem, sum(bin(common(b)).count("1") for b in others),
-               [c("AL", 32 * r + 4 * k, 32 * r + 4 * k + 4) for k in range(N) if k != q])
+        arrive(sem, sum(bin(common(b)).count("1") for b in others), slots)
 
     load("s", c("MI", 0, 60), T.mg[:])
+    load("s", c("DI", 0, 96), T.dam[:, 0:96])
     load("s", c("AI", 0, 1), T.aim0[:])
     lc = _cuts(LOAD)
     load("y", c("SI", 0, 288), T.sire[:])
     for a, b in lc:
         load("y", c("TI", a, b), T.trait[:, a:b])
-    load("y", c("DI", 0, 416), T.dam[:])
+    load("y", c("DI", 96, 416), T.dam[:, 96:416])
+    s1, s2 = ST[1], ST[2]
     iota(c("PI", 0, 1), [[0, 1]], 0, 1)
     iota(c("AR", 0, 16), [[1, 16]], 0, 0, True)
     iota(c("BASE", 0, 48), [[96, 4], [0, 12]], 0, 0)
-    iota(c("ID", 0, 128), [[-1, 128]], 0, 1, True)
-    iota(c("EF", 0, 128), [[-1, 2], [-2, 64]], 0, 1, True)
-    iota(c("UF", 0, 10), [[16, 10]], 23, 0, True)
-    iota(c("IO", 0, A), [[1, A]], 0, 0, True)
-    iota(c("X", F, F + E), [[0, E]], 0, 0, True)
-    iota(c("X", ST[2] - E, ST[2]), [[0, E]], 0, 0, True)
-    iota(c("RS", 0, 8), [[0, 8]], 0, 0, True)
-    issue("v", lambda: g.vector.memset(T.WB[:, 0:144], 0.0), [c("WB", 0, 144)], [])
+    iota(c("X", s2 - E, s2), [[0, E]], 0, 0, True)
+    iota(c("ID", 0, 160), [[-1, 160]], 16, 1, True)
+    iota(c("X", F, s1), [[0, E]], 0, 0, True)
+    iota(c("WB", 0, 144), [[0, 144]], 0, 0, True)
     ts(c("PJ", 0, 1), c("PI", 0, 1), 15, Op.bitwise_and)
     ts(c("PJ", 1, 2), c("PI", 0, 1), 4, Op.arith_shift_right)
     copy(c("PF", 0, 2), c("PJ", 0, 2))
@@ -229,78 +258,102 @@ def rank_program(g, core, T, topo):
     ts(c("LI", 0, 48), c("MI", 12, 60), 15, Op.bitwise_and)
     copy(c("LU", 0, 48), c("LI", 0, 48))
     ts(c("HI", 0, 48), c("MI", 12, 60), 4, Op.arith_shift_right)
-    copy(c("MU", 0, 12), c("MI", 0, 12))
     tt(c("HJ", 0, 48), c("HI", 0, 48), c("BASE", 0, 48), Op.add)
     copy(c("HU", 0, 48), c("HJ", 0, 48))
-    act(c("MK", 0, 768), ind(c("I16", 0, 16), c("LU", 0, 48)))
+    act(c("MK", 0, E), ind(c("I16", 0, 16), c("LU", 0, 12)))
+    act(c("MK", E, 768), ind(c("I16", 0, 16), c("LU", 12, 48)))
+    tt(c("Z", 576, 768), ind(c("DI", 0, 96), c("HU", 0, 12)), c("MK", 0, E), Op.mult)
+    copy(c("MU", 0, 12), c("MI", 0, 12))
     own, nown = c("CC", 0, 1), c("CC", 1, 2)
-    act(own, c("I16", 2 * q, 2 * q + 1), Fn.Identity, c("I16", 2 * q + 1, 2 * q + 2))
-    act(c("CC", 4, 5), pm, Fn.Identity, -1024.0, 128.0)
-    act(c("JK", 0, 128), c("ID", 0, 128), Fn.Abs)
-    act(c("JK", 128, 256), c("EF", 0, 128), Fn.Abs)
-    act(nown, own, Fn.Identity, 1.0, -1.0)
-    act(c("DM", 0, 16), c("I16", 0, 16), Fn.Identity, 0.0, own)
-    act(c("ID", 0, 128), c("JK", 0, 128), Fn.Relu, 1.0, -1.0)
-    act(c("EB", 0, 128), c("JK", 128, 256), Fn.Relu, 1.0, -1.0)
-    act(c("WD", 0, 144), c("WB", 0, 144), Fn.Identity, 0.0, c("I16", (2 * q + 2) % 16, (2 * q + 2) % 16 + 1))
-    for r, eps in enumerate((128.0, 256.0)):
-        act(c("CC", 2 + r, 3 + r), pm, Fn.Identity, 15.0 / (8 * eps), -1.0 / (8 * eps))
     t0, h0 = c("TC", 0, 1), c("TH", 0, 1)
     copy(t0, c("AI", 0, 1))
-    ts(h0, t0, 0.5, Op.mult)
+    act(h0, t0, Fn.Identity, 0.0, 0.5)
+    tt(c("Z", 0, 576), ind(c("SI", 0, 288), c("HU", 0, 36)), c("MK", 0, 576), Op.mult)
+    fold16(c("BA", 0, 48), "WB", "Z", 0, 768)
+    act(own, c("I16", 2 * q, 2 * q + 1), Fn.Identity, c("I16", 2 * q + 1, 2 * q + 2))
+    act(c("J4", 0, 160), c("ID", 0, 160), Fn.Abs)
+    act(nown, own, Fn.Identity, 1.0, -1.0)
+    act(c("DM", 0, 16), c("I16", 0, 16), Fn.Identity, 0.0, own)
+    act(c("ID", 0, 160), c("J4", 0, 160), Fn.Relu, 1.0, -1.0)
+    act(c("HP", 0, 128), c("J4", 16, 144), Fn.Relu, 0.5, -1.0)
+    act(c("HN", 0, 128), c("HP", 0, 128), Fn.Identity, 0.0, -1.0)
+    act(c("WD", 0, 144), c("WB", 0, 144), Fn.Identity, 0.0, c("I16", (2 * q + 2) % 16, (2 * q + 2) % 16 + 1))
+    ma, mb = c("I16", (2 * q + 2) % 16, (2 * q + 2) % 16 + 1), c("I16", (2 * q + 3) % 16, (2 * q + 3) % 16 + 1)
+    act(c("WF", 0, 144), c("WB", 0, 144))
+    act(c("CC", 6, 7), ma, Fn.Identity, mb)
+    act(c("CC", 7, 8), mb, Fn.Identity, ma, -1.0)
+    act(c("WH", 0, 144), c("WB", 0, 144), Fn.Identity, 0.0, c("CC", 6, 7))
+    for r, eps in enumerate((128.0, 256.0)):
+        act(c("CC", 2 + r, 3 + r), pm, Fn.Identity, 0.0, 1.0 / (8 * eps))
+    iota(c("EF", 0, 128), [[-1, 2], [-2, 64]], 0, 1, True)
+    iota(c("UF", 0, 10), [[16, 10]], 23, 0, True)
+    iota(c("RS", 0, 8), [[0, 8]], 0, 0, True)
+    act(c("CC", 4, 5), pm, Fn.Identity, -1024.0, 128.0)
+    act(c("EF", 0, 128), c("EF", 0, 128), Fn.Abs)
+    act(c("EB", 0, 128), c("EF", 0, 128), Fn.Relu, 1.0, -1.0)
+    ts(c("CC", 5, 6), c("CC", 4, 5), 4.0, Op.mult, c("CC", 4, 5), Op.min)
+    ts(c("UO", 0, 10), c("UF", 0, 10), c("CC", 5, 6), Op.add, 1031.0, Op.min)
 
     def founders(k):
         a, b = lc[k]
         copy(c("X", a, b), c("TI", a, b))
         act(c("TA", a, b), c("X", a, b), Fn.Abs, t0, -1.0)
+        if a < NV:
+            act(c("X2", a, min(b, NV)), c("X", a, min(b, NV)), Fn.Identity, 0.0, 2.0)
 
-    tt(c("Z", 0, 576), ind(c("SI", 0, 288), c("HU", 0, 36)), c("MK", 0, 576), Op.mult)
-    fold16(c("PM", 0, 36), "WB", "Z", 0, 576)
     copy(c("SU", 0, 288), c("SI", 0, 288))
-    for k in range(len(lc) - 1):
+    founders(0)
+    for a in range(0, A, 384):
+        iota(c("IO", a, a + 384), [[1, 384]], a, 0)
+    founders(1)
+    copy(c("CL", 0, 48), c("BA", 0, 48))
+    for k in range(2, len(lc) - 1):
         founders(k)
     copy(c("SE0", 0, E), ind(c("TI", 0, F), c("MU", 0, 12)))
-    send(c("SE0", 0, E), c("TI", F, F + E))
+    send(c("SE0", 0, E), c("GU", 0, E))
     founders(len(lc) - 1)
 
-    s1, s2 = ST[1], ST[2]
-
-    def split(out, o, n, wv, ws, lst, l0):
-        copy(c(out, o, o + n), ind(wv, c(lst, l0, l0 + n // 16)))
-        act(c(out, o + n, o + A), ind(ws, c(lst, l0 + n // 16, l0 + 96)))
-
-    copy(c("CL", 0, 36), c("PM", 0, 36))
-    tt(c("Z", 576, 1344), ind(c("DI", 0, 416), c("HU", 0, 48)), c("MK", 0, 768), Op.mult)
-    fold16(c("PN", 0, 48), "WB", "Z", 576, 768)
-    split("X", s1, P1[0], c("TI", 0, F), c("X", 0, F), "SU", 0)
-    copy(c("SE1", 0, E), ind(c("TI", 0, F), c("CL", 0, 12)))
-    send(c("SE1", 0, E), c("MD", A + E, A + 2 * E))
-    iota(c("SEG", 0, 512), [[0, 32], [32767, 16]], 0, 0, True)
+    xf, xg = c("X", 0, F), c("X", 0, s1)
+    act(c("SE1", 0, E), ind(xf, c("CL", 0, 12)))
+    send(c("SE1", 0, E), c("GP", 0, E))
+    iota(c("SEG", 0, 512), [[0, 32], [-32767, 16]], 1, 0, True)
+    n = P1[0]
+    copy(c("X", s1, s1 + n), ind(xf, c("SU", 0, n // 16)))
+    act(c("X", s1 + n, s1 + A), ind(xf, c("SU", n // 16, 96)))
+    tt(c("Z", 768, 1344), ind(c("DI", 0, 416), c("HU", 12, 48)), c("MK", E, 768), Op.mult)
+    fold16(c("BB", 12, 48), "WB", "Z", 768, 576)
     copy(c("DU", 0, 416), c("DI", 0, 416))
-    split("X", s2, P1[1], c("X", 0, s1 + A), c("X", 0, s1 + A), "SU", 96)
-    act(c("HR", 0, A), c("X", s1, s1 + A), Fn.Abs, h0, -0.5)
-    copy(c("CL", 36, 84), c("PN", 0, 48))
+    copy(c("X", s2, s2 + X2V), ind(c("X", 0, s1 + A), c("SU", 96, 96 + X2V // 16)))
+    act(c("X", s2 + X2V, s2 + A), ind(c("X", 0, s1 + A), c("SU", 96 + X2V // 16, 192)))
 
-    wi = c("TI", 0, s1)
-    copy(c("SE1", E, 2 * E), ind(wi, c("CL", 36, 48)))
-    send(c("SE1", E, 2 * E), c("MD", A, A + E))
-    copy(c("X", F, s1), c("TI", F, s1))
-    n, m = P1[2], (P1[2] + A) // 64 * 32
-    copy(c("MD", n, m), ind(wi, c("DU", n // 16, m // 16)))
-    act(c("MD", 0, n), ind(c("X", 0, s1), c("DU", 0, n // 16)))
-    copy(c("MD", m, A), ind(wi, c("DU", m // 16, 96)))
+    def x3(k):
+        a, b = ([0] + X3P)[k], X3P[k]
+        (act if k else copy)(c("X3", a, b), ind(c("X", 0, s2 + A), c("SU", 192 + a // 16, 192 + b // 16)))
+
+    act(c("AV", 0, A), c("X", s1, s1 + A), Fn.Abs, h0, -0.5)
+    copy(c("X", F, s1), c("GU", 0, E))
+    copy(c("SE1", E, 2 * E), ind(xg, c("CL", 36, 48)))
+    send(c("SE1", E, 2 * E), c("GP", E, 2 * E))
+    n, m = P1[1], (P1[1] + A) // 64 * 32
+    copy(c("MD", n, m), ind(xg, c("DU", n // 16, m // 16)))
+    act(c("MD", 0, n), ind(xg, c("DU", 0, n // 16)))
+    copy(c("MD", m, A), ind(xg, c("DU", m // 16, 96)))
     act(c("TA", s1, s1 + m), c("MD", 0, m), Fn.Abs, h0, -0.5)
     act(c("TA", s1 + m, s1 + A), c("MD", m, A), Fn.Abs, h0, -0.5)
-    copy(c("X3", 0, P1[3]), ind(c("X", 0, s2 + A), c("SU", 192, 192 + P1[3] // 16)))
-    tt(c("TA", s1, s1 + m), c("TA", s1, s1 + m), c("HR", 0, m), Op.add)
+    copy(c("CL", 48, 84), c("BB", 12, 48))
+    x3(0)
+    tt(c("TA", s1, s1 + m), c("TA", s1, s1 + m), c("AV", 0, m), Op.add)
     act(c("TA", F, s1), c("X", F, s1), Fn.Abs, t0, -1.0)
-    tt(c("TA", s1 + m, s1 + A), c("TA", s1 + m, s1 + A), c("HR", m, A), Op.add)
-    act(c("HR", A, A + E), c("MD", A + E, A + 2 * E), Fn.Abs, h0, -0.5)
-    act(c("X3", P1[3], P1[4]), ind(c("X", 0, s2 + A), c("SU", 192 + P1[3] // 16, 192 + P1[4] // 16)))
+    x3(1)
+    act(c("GT", 0, 2 * E), c("GP", 0, 2 * E), Fn.Abs, h0, -0.5)
+    tt(c("TA", s1 + m, s1 + A), c("TA", s1 + m, s1 + A), c("AV", m, A), Op.add)
+    hp, hn = c("HP", 0, 128), c("HN", 0, 128)
+    for name, w, n in (("DL", hn, A), ("AV", hp, NP)):
+        for a in range(0, n, 512):
+            mm(c(name, a, a + 512), [(hp, c("X", s1 + a, s1 + a + 512)), (w, c("MD", a, a + 512))])
 
-    def first_ghosts():
-        act(c("TA", s1 + A, s2), c("MD", A, A + E), Fn.Abs, h0, -0.5)
-        tt(c("TA", s1 + A, s2), c("TA", s1 + A, s2), c("HR", A, A + E), Op.add)
+    def ghosts1(tb):
+        tt(c(tb, s1 + A, s2), c("GT", 0, E), c("GT", E, 2 * E), Op.add)
 
     nse = [0]
 
@@ -313,7 +366,7 @@ def rank_program(g, core, T, topo):
         act(c("JK", cut, n), c("R1", cut, n), Fn.Sign, big, -1.0, c("CN", 1, 2))
         ts(c("CN", 2, 3), c("R1", cut - 1, cut), big, Op.is_lt, float(cut), Op.mult)
         ts(c("IU", 0, 1), c("CN", 2, 3), c("CN", 0, 1), Op.max, c("CN", 1, 2), Op.add)
-        tt(c("G16", 16 * r, 16 * r + 16), ind(win, c("IU", 0, 1)), c("DM", 0, 16), Op.mult)
+        tt(c("AL", 48 * r, 48 * r + 16), ind(win, c("IU", 0, 1)), c("DM", 0, 16), Op.mult)
         send_aims(r)
 
     def least_step(tb, s, a, b, cut):
@@ -329,9 +382,7 @@ def rank_program(g, core, T, topo):
         o = (e - 1) * 96
         sb = sendbuf()
         sl, dl = c("CL", 12 * (e - 1), 12 * e), c("CL", 36 + 12 * (e - 1), 36 + 12 * e)
-        va = cuts[0][1] if newest else GEN_VA
-        act(c("PE", 0, E), ind(ws, sl))
-        copy(c("AB", 0, va), ind(ws, c("SU", o, o + va // 16)))
+        copy(c("PE", 0, E), ind(ws, sl))
         if pre:
             pre()
         if newest:
@@ -341,13 +392,11 @@ def rank_program(g, core, T, topo):
             ts(sb, c("QE", 0, E), 0.5, Op.mult)
         send(sb, c(tb, s + A, s + A + E))
         for a, b in cuts:
-            if b > va:
-                a = max(a, va)
-                act(c("AB", a, b), ind(ws, c("SU", o + a // 16, o + b // 16)))
+            act(c("AB", a, b), ind(ws, c("SU", o + a // 16, o + b // 16)))
         if newest:
-            act(c("X3", P1[4], A), ind(c("X", 0, s2 + A), c("SU", 192 + P1[4] // 16, 288)))
+            x3(2)
         cut = cuts[-1][0]
-        for k, (a, b) in enumerate(cuts):
+        for a, b in cuts:
             du = c("DU", o + a // 16, o + b // 16)
             if newest:
                 tt(c(tb, s + a, s + b), ind(wd, du), c("AB", a, b), Op.add)
@@ -355,140 +404,148 @@ def rank_program(g, core, T, topo):
                     least_step(tb, s, 0 if b == cut else a, b, cut)
             else:
                 tt(c("AB", a, b), ind(wd, du), c("AB", a, b), Op.add)
-                h = min(b, A - GEN_VH)
-                act(c(tb, s + a, s + h), c("AB", a, h), Fn.Identity, 0.0, 0.5)
-                if h < b:
-                    ts(c(tb, s + h, s + b), c("AB", h, b), 0.5, Op.mult)
+                if b < A:
+                    act(c(tb, s + a, s + b), c("AB", a, b), Fn.Identity, 0.0, 0.5)
+                else:
+                    ts(c(tb, s + a, s + b), c("AB", a, b), 0.5, Op.mult)
         return cut
 
     def sires_out(r):
-        act(c("YS", 64 * r, 64 * r + 64), c("PM", 0, 64), Fn.Identity, float(ST[3 + r]))
+        fold16(c("BB", 128, 192), ("WD", "WH")[r], ("PG", "PH")[r], 0, D)
+        act(c("YS", 64 * r, 64 * r + 64), c("BB", 128, 192), Fn.Identity, float(ST[3 + r]))
 
     def choose(tb, r):
         e = 3 + r
         s, n = ST[e], (A if r == 0 else D)
-        eps = 128.0 if r == 0 else 256.0
         x = c(tb, s, s + n)
         ce = c("CC", 2 + r, 3 + r)
         scan(c("R2", 0, n), x, x, 1.0e9, Op.min, Op.min)
         o = 288 + 64 * r
-        act(c("K", 0, D), ind(c(tb, 0, ST[e + 1]), c("DU", o, o + 64)), Fn.Identity, ce, 0.125)
-        act(c("JK", 0, n), c("R2", 0, n), Fn.Sign, c("R2", n - 1, n), -1.0, c("CN", 4, 5))
+        kv = KV[r]
+        ts(c("K", 0, kv), ind(c(tb, 0, ST[e + 1]), c("DU", o, o + kv // 16)), -0.125, Op.mult, ce, Op.add)
+        act(c("K", kv, D), ind(c(tb, 0, ST[e + 1]), c("DU", o + kv // 16, o + 64)), Fn.Identity, ce, -0.125)
+        act(c("YF", 0, n), c("R2", 0, n), Fn.Sign, c("R2", n - 1, n), -1.0, c("CN", 4, 5))
         if r == 0:
-            ts(c("CC", 5, 6), c("CC", 4, 5), 4.0, Op.mult, c("CC", 4, 5), Op.min)
-            ts(c("UO", 0, 10), c("UF", 0, 10), c("CC", 5, 6), Op.add, 1031.0, Op.min)
-            act(c("X", s2 - E, s2), c("MD", A + E, A + 2 * E))
-            act(c("X2", 0, NV), c("X", 0, NV), Fn.Identity, 0.0, 2.0)
-        else:
-            sires_out(0)
-        for h in range(2):
-            def fn():
-                for u in range(4 * h, 4 * h + 4):
-                    last = g.tensor.transpose(T.PT[:, 128 * u:128 * u + 128], T.K[:, u:D:8], T.ID[:, 0:128])
-                return last
-            issue("p", fn, [c("PT", 512 * h, 512 * h + 512)], [c("K", 0, D), c("ID", 0, 128)])
-        for h in range(2):
-            scan(c("RS", 8 + 512 * h, 520 + 512 * h), c("SEG", 0, 512), c("PT", 512 * h, 512 * h + 512), 0.0, Op.min, Op.max)
-        ts(c("UI", 0, 144), ind(c("RS", 0, 1032), c("UO", 0, 9)), 8 * eps, Op.mult)
+            for a in range(0, A, 512):
+                act(c("DL", a, a + 512), c("DL", a, a + 512), Fn.Abs)
+            tt(c("MD", NP, A), c("MD", NP, A), c("X", s1 + NP, s1 + A), Op.add)
+        ts(c("IU", 2 + 2 * r, 3 + 2 * r), c("CN", 4, 5), -1.0, Op.mult)
+
+    def rows(r):
         bu = c("IU", 2 + 2 * r, 3 + 2 * r)
-        ts(bu, c("CN", 4, 5), -1.0, Op.mult)
-        ts(c("UJ", 0, 144), c("UI", 0, 144), 15, Op.bitwise_and)
-        copy(c("UB", 0, 144), c("UJ", 0, 144))
-        mm(c("PM", 0, 64), [(c("UB", 8, 136), c("EB", 0, 64)), (c("UB", 0, 128), c("EB", 64, 128))])
+        for h, bank in enumerate(("BA", "BB")):
+            def fn(h=h, bank=bank):
+                for u in range(4):
+                    last = g.tensor.transpose(c(bank, 128 * u, 128 * u + 128)[0], T.K[:, 4 * h + u:D:8], T.ID[:, 16:144])
+                return last
+            issue("p", fn, [c(bank, 0, 512)], [c("K", 0, D), c("ID", 0, 160)])
+            scan(c("RS", 8 + 512 * h, 520 + 512 * h), c("SEG", 0, 512), c(bank, 0, 512), 0.0, Op.max, Op.min)
+        act(c("UB", 0, 144), ind(c("RS", 0, 1032), c("UO", 0, 9)), Fn.Identity, 0.0, 1024.0 * (r + 1))
+        mm(c("BB", 0, 64), [(c("UB", 8, 136), c("EB", 0, 64)), (c("UB", 0, 128), c("EB", 64, 128))])
         ml = c("MM", 64 * r, 64 * r + 64)
-        p16 = c("P16", 32, 48)
         if r == 0:
-            ts(c("P16", 0, 16), ind(c("X3", 0, A), bu), own, Op.mult)
-            ts(c("P16", 16, 32), ind(c("IO", 0, A), bu), nown, Op.mult)
-            ts(c("DI", 288, 352), c("PM", 0, 64), -1.0, Op.mult, 15.0, Op.add)
-            tt(p16, c("P16", 0, 16), c("P16", 16, 32), Op.add)
-            copy(ml, c("DI", 288, 352))
-            tt(c("ZM", 0, E), ind(c("DI", 0, 352), c("HU", 36, 48)), c("MK", 576, 768), Op.mult)
-            fold16(c("PN", 0, 12), "WB", "ZM", 0, E)
+            ts(c("P16", 48, 64), ind(c("IO", 0, A), bu), nown, Op.mult)
+            act(c("P16", 64, 80), ind(c("X3", 0, A), bu), Fn.Identity, 0.0, own)
+            tt(c("P16", 0, 16), c("P16", 48, 64), c("P16", 64, 80), Op.add)
         else:
-            copy(p16, ind(c("IO", 0, A), bu))
-            ts(ml, c("PM", 0, 64), -1.0, Op.mult, 15.0, Op.add)
+            copy(c("P16", 16, 32), ind(c("IO", 0, A), bu))
+            act(c("PB", 0, 16), c("P16", 16, 32))
+            act(c("P16", 48, 64), c("P16", 16, 32), Fn.Identity, 0.0, mb)
+            act(c("P16", 64, 80), c("PB", 0, 16), Fn.Identity, 0.0, c("CC", 7, 8))
+            tt(c("P16", 32, 48), c("P16", 48, 64), c("P16", 64, 80), Op.add)
+        copy(c("UJ", 0, 64), c("BB", 0, 64))
+        ts(c("DI", 288, 352), c("UJ", 0, 64), 15, Op.bitwise_and)
+        copy(ml, c("DI", 288, 352))
+        if r == 0:
+            tt(c("ZM", 0, E), ind(c("DI", 0, 352), c("HU", 36, 48)), c("MK", 576, 768), Op.mult)
+            fold16(c("BB", 64, 76), "WF", "ZM", 0, E)
 
     def payload(r, part):
-        pg, p16 = ("PG" if r == 0 else "PH"), c("P16", 32, 48)
+        pg, p16, n = ("PG" if r == 0 else "PH"), c("P16", 32 * r, 32 * r + 16), PVR[r]
         if part == 0:
-            copy(c(pg, 0, PV), ind(p16, c("MM", 64 * r, 64 * r + PV // 16)))
+            copy(c(pg, 0, n), ind(p16, c("MM", 64 * r, 64 * r + n // 16)))
         else:
-            act(c(pg, PV, D), ind(p16, c("MM", 64 * r + PV // 16, 64 * r + 64)))
-            fold16(c("PM", 0, 64), "WD", pg, 0, D)
+            act(c(pg, n, D), ind(p16, c("MM", 64 * r + n // 16, 64 * r + 64)))
 
     def start_round(tb, r):
-        t, h = c("TC", r, r + 1), c("TH", r, r + 1)
-        al = c("AL", 32 * (r - 1), 32 * r)
-        act(c("JK", 0, 32), al, Fn.Identity, 0.0, 1.0, t)
-        act(c("JK", 32, 64), al, Fn.Identity, 0.0, 0.5, h)
-        act(c(tb, s1, s2), c("MD", 0, A + E), Fn.Abs, h, -0.5)
-        act(c("HR", 0, A + E), c("X", s1, s2), Fn.Abs, h, -0.5)
+        t, h, tv = c("TC", r, r + 1), c("TH", r, r + 1), c("TV", r, r + 1)
+        al = c("AL", 48 * (r - 1), 48 * (r - 1) + 44)
+        act(c("J3", 48 * (r - 1), 48 * (r - 1) + 44), al, Fn.Identity, 0.0, 1.0, t)
+        issue("v", lambda: g.vector.tensor_reduce(tv[0], al[0], Ax.X, Op.add), [tv], [al])
+        act(c(tb, s1, s1 + NP), c("AV", 0, NP), Fn.Abs, t, -1.0)
+        act(h, t, Fn.Identity, 0.0, 0.5)
+        act(c(tb, s1 + NP, s1 + A), c("MD", NP, A), Fn.Abs, t, -0.5)
+        for a in range(0, NV, 512):
+            ts(c("BA", 0, 512), c("X2", a, a + 512), tv, Op.subtract, tv, Op.max)
+            tt(c(tb, a, a + 512), c("BA", 0, 512), c("X", a, a + 512), Op.subtract)
+        act(c("GT", 0, 2 * E), c("GP", 0, 2 * E), Fn.Abs, h, -0.5)
         act(c(tb, NV, s1), c("X", NV, s1), Fn.Abs, t, -1.0)
-        ts(c("PT", 0, NV), c("X2", 0, NV), t, Op.subtract, t, Op.max)
-        tt(c(tb, 0, NV), c("PT", 0, NV), c("X", 0, NV), Op.subtract)
+        tt(c(tb, s1, s1 + A), c(tb, s1, s1 + A), c("DL", 0, A), Op.max)
+        ghosts1(tb)
         if r == 1:
-            copy(c("CM", 0, 12), c("PN", 0, 12))
-        tt(c(tb, s1, s2), c(tb, s1, s2), c("HR", 0, A + E), Op.add)
+            copy(c("CM", 0, 12), c("BB", 64, 76))
 
     def fourth(tb, r):
         s = ST[4]
         wd = c(tb, 0, s)
-        payload(r - 1, 0)
+        if r == 1:
+            payload(0, 0)
         t16 = c("T16", 16 * r, 16 * r + 16)
         ts(t16, ind(c(tb, ST[3], ST[3] + A), c("IU", 2, 3)), 0.5, Op.mult)
         act(c("QE", 0, E), ind(wd, c("CL", 72, 84)), Fn.Identity, 0.0, 0.5)
         sb = sendbuf()
         cuts = _cuts(G4)
-        a, b = cuts[0]
-        h = (a + b) // 64 * 32
-        ts(c("AB", a, h), ind(wd, c("DU", 288 + a // 16, 288 + h // 16)), 0.5, Op.mult)
+        ts(c("AB", 0, G4V), ind(wd, c("DU", 288, 288 + G4V // 16)), 0.5, Op.mult)
         tt(sb, ind(t16, c("CM", 0, 12)), c("QE", 0, E), Op.add)
         send(sb, c(tb, s + D, s + D + E))
         cut = cuts[-1][0]
         for k, (a, b) in enumerate(cuts):
-            lo = h if k == 0 else a
+            lo = G4V if k == 0 else a
             act(c("AB", lo, b), ind(wd, c("DU", 288 + lo // 16, 288 + b // 16)), Fn.Identity, 0.0, 0.5)
-        payload(r - 1, 1)
+        if r == 1:
+            payload(0, 1)
         for k, (a, b) in enumerate(cuts):
             tt(c(tb, s + a, s + b), ind(t16, c("MM", a // 16, b // 16)), c("AB", a, b), Op.add)
             if r == 1 and b >= cut:
                 least_step(tb, s, 0 if b == cut else a, b, cut)
+            if r == 2:
+                act(c("YF", a, b), c(tb, s + a, s + b), Fn.Identity, 65535.0, -1.0)
+                store(T.yf[:, a:b], c("YF", a, b))
         return cut
 
-    generation("TA", 2, False, first_ghosts)
+    generation("TA", 2, False, lambda: ghosts1("TA"))
     cut = generation("TA", 3, True)
     least_tail(A, cut, 0, c("X3", 0, A))
     choose("TA", 0)
+    rows(0)
     start_round("TB", 1)
     generation("TB", 2, False)
     generation("TB", 3, False)
     cut = fourth("TB", 1)
     least_tail(D, cut, 1, c("PG", 0, D))
     choose("TB", 1)
+    rows(1)
     start_round("TA", 2)
     store(T.yt[:], c("TC", 1, 3))
     generation("TA", 2, False)
+    sires_out(0)
     generation("TA", 3, False)
     fourth("TA", 2)
     t16 = c("T16", 48, 64)
     ts(t16, ind(c("TA", ST[4], ST[4] + D), c("IU", 4, 5)), -0.5, Op.mult)
-    act(c("YF", 0, 512), c("TA", ST[4], ST[4] + 512), Fn.Identity, 65535.0, -1.0)
-    ts(c("YF", 512, D), c("TA", ST[4] + 512, ST[4] + D), -1.0, Op.mult, 65535.0, Op.add)
-    store(T.yf[:, 0:D], c("YF", 0, D))
+    payload(1, 0)
+    payload(1, 1)
     wd = c("TA", 0, ST[5])
     cuts = _cuts(G5)
     for k, (a, b) in enumerate(cuts):
         if k == 0:
-            h = (a + b) // 64 * 32
-            ts(c("AB", a, h), ind(wd, c("DU", 352 + a // 16, 352 + h // 16)), -0.5, Op.mult, 65535.0, Op.add)
-            a = h
+            ts(c("AB", a, G5V), ind(wd, c("DU", 352 + a // 16, 352 + G5V // 16)), -0.5, Op.mult, 65535.0, Op.add)
+            a = G5V
         act(c("AB", a, b), ind(wd, c("DU", 352 + a // 16, 352 + b // 16)), Fn.Identity, 65535.0, -0.5)
-    sires_out(1)
     for k, (a, b) in enumerate(cuts):
         tt(c("YF", D + a, D + b), ind(t16, c("MM", 64 + a // 16, 64 + b // 16)), c("AB", a, b), Op.add)
         store(T.yf[:, D + a:D + b], c("YF", D + a, D + b))
         if k == 0:
+            sires_out(1)
             store(T.ys[:], c("YS", 0, 128))
-    for sem in sorted(count):
-        wait("y" if sem == "stored" else "g", sem, count[sem])
+    emit()

from concourse.bass import DstId, RemoteDMATransfer
from concourse.mybir import AluOpType as Op, ActivationFunctionType as Fn, AxisListType as Ax

F, A, D, E = 3072, 1536, 1024, 192
ST = [0, 3264, 4992, 6720, 8448, 9664]
NV = 1024
NP = 1024

f32, i32, u16, bf = "float32", "int32", "uint16", "bfloat16"


def _sb(n, t=f32):
    return ("sbuf", [128, n], t)


SCRATCH = {
    "TI": _sb(3072, i32), "IO": _sb(1536, i32), "SI": _sb(288, i32), "DI": _sb(416, i32), "MI": _sb(64, i32), "AI": _sb(4, i32),
    "SU": _sb(288, u16), "DU": _sb(416, u16), "MU": _sb(16, u16), "HU": _sb(48, u16), "LU": _sb(48, u16),
    "CL": _sb(96, u16), "HI": _sb(48, i32), "HJ": _sb(48, i32), "LI": _sb(48, i32), "BASE": _sb(48, i32),
    "PI": _sb(4, i32), "PJ": _sb(4, i32), "PF": _sb(4), "AR": _sb(16), "I16": _sb(16), "DM": _sb(16), "CC": _sb(8),
    "WB": _sb(144), "WD": _sb(144), "ID": _sb(160), "EF": _sb(128), "EB": _sb(128), "UF": _sb(16), "UO": _sb(16, u16),
    "SEG": _sb(512), "HP": _sb(128), "HN": _sb(128), "TC": _sb(4), "TH": _sb(4), "TV": _sb(4),
    "X": _sb(6528), "X3": _sb(1536), "MD": _sb(1536), "X2": _sb(NV), "TA": _sb(9664), "TB": _sb(9664), "AB": _sb(1536),
    "R1": _sb(1536), "R2": _sb(1536), "RS": _sb(1032), "K": _sb(1024), "Z": _sb(1344), "MK": _sb(768),
    "PG": _sb(1024), "PH": _sb(1024, bf), "JK": _sb(1536, bf), "J3": _sb(96), "J4": _sb(160),
    "SE0": _sb(192, u16), "GU": _sb(192, u16), "SE1": _sb(384), "GP": _sb(384), "GT": _sb(384),
    "SE": _sb(192 * 8), "PE": _sb(192), "QE": _sb(192),
    "AL": _sb(96), "CN": _sb(16), "IU": _sb(16, u16), "T16": _sb(64), "P16": _sb(80),
    "UJ": _sb(64, i32), "UB": _sb(144), "MM": _sb(128, u16), "ZM": _sb(192, bf), "WF": _sb(144, bf), "WH": _sb(144, bf),
    "PB": _sb(16, bf), "CM": _sb(16, u16),
    "YF": _sb(2048), "YS": _sb(128),
    "HR": ("psum", [128, 2048], f32), "PT": ("psum", [128, 2048], f32),
}
PSUM = ("HR", "PT")
PART = {"AV": ("HR", 0), "DL": ("PT", 0), "BA": ("HR", 1536), "BB": ("PT", 1536)}
SEMAPHORES = (["qv", "qs", "qp", "qg", "sent", "stored"] + ["ld%d" % k for k in range(10)]
              + ["ar%d" % k for k in range(11)] + ["aim0s", "aim1s"])

LOAD = [896, 896, 768, 512]
GEN = [512, 576, 448]
NEW = [448, 704, 384]
P1 = [768, 512]
X2V = 896
X3P = [128, 640, 1536]
PVR = [384, 256]
G4 = [384, 384, 256]
G4V = 192
G5 = [256, 448, 320]
G5V = 128
KV = [384, 512]
DAG = {}
ORDER = [
    0, 2, 1, 5, 3, 4, 6, 7, 8, 9, 13, 10, 15, 50, 48, 11, 49, 14, 12, 61, 62, 63, 60, 16, 17, 18, 35, 51, 19, 54, 20, 21, 23, 22, 24, 30, 25,
    29, 39, 44, 38, 34, 37, 26, 52, 27, 36, 53, 31, 42, 28, 64, 40, 43, 46, 41, 65, 32, 57, 56, 33, 68, 70, 73, 83, 67, 79, 81, 58, 59, 69,
    80, 75, 85, 86, 84, 82, 71, 72, 87, 88, 92, 91, 94, 93, 96, 99, 95, 74, 98, 102, 108, 76, 78, 89, 77, 90, 101, 109, 110, 111, 112, 115,
    114, 119, 116, 117, 120, 118, 55, 121, 122, 97, 123, 100, 127, 128, 129, 45, 130, 113, 131, 124, 125, 132, 133, 134, 135, 136, 138, 137,
    139, 140, 141, 126, 144, 142, 143, 103, 107, 105, 104, 145, 147, 66, 148, 149, 146, 154, 152, 106, 155, 150, 153, 166, 169, 170, 175,
    168, 167, 151, 171, 158, 172, 178, 173, 177, 174, 176, 180, 181, 182, 186, 190, 185, 187, 188, 159, 156, 189, 191, 157, 192, 161, 193,
    162, 194, 183, 184, 160, 195, 196, 197, 198, 199, 200, 201, 164, 202, 204, 165, 206, 163, 207, 179, 203, 47, 205, 209, 211, 210, 215,
    216, 212, 213, 214, 219, 220, 221, 217, 218, 222, 223, 224, 225, 233, 226, 208, 227, 228, 232, 229, 230, 231, 234, 236, 237, 238, 250,
    253, 254, 252, 259, 260, 235, 239, 251, 242, 255, 256, 257, 261, 258, 262, 264, 265, 266, 267, 268, 270, 269, 274, 271, 240, 272, 276,
    241, 247, 277, 278, 275, 244, 273, 243, 280, 281, 282, 245, 285, 288, 286, 290, 287, 289, 291, 279, 292, 283, 284, 293, 295, 300, 294,
    246, 296, 297, 248, 303, 301, 302, 249, 306, 309, 312, 313, 298, 299, 315, 304, 314, 310, 307, 316, 319, 321, 317, 322, 263, 305, 311,
    308, 324, 318, 326, 320, 323, 325, 327]


def _cuts(plan):
    out, a = [], 0
    for n in plan:
        out.append((a, a + n))
        a += n
    return out


def rank_program(g, core, T, topo):
    q = T.rank_of(core)
    if q is None:
        return
    N = len(T.cores)
    others = [T.cores[(q + k) % N] for k in range(1, N)]
    queue = {"v": g.vector, "s": g.scalar, "p": g.tensor, "g": g, "y": g.sync}
    count = {}
    know = {k: {} for k in queue}
    clock = {}
    log = {}
    ops = []
    DAG["ops"] = ops

    def c(name, a, b, s=None):
        if name in PART:
            name, a, b = PART[name][0], a + PART[name][1], b + PART[name][1]
        ap = T[name][:, a:b] if s is None else T[name][:, a:b:s]
        if name in PSUM:
            a, b = a // 512 * 512, -(-b // 512) * 512
        return (ap, [(name, a, b)])

    def ind(win, off):
        return (win[0].indirect(off[0]), win[1] + off[1])

    def val(x):
        return x[0] if isinstance(x, tuple) else x

    def regs(xs):
        return [r for x in xs if isinstance(x, tuple) for r in x[1]]

    def wait(e, sem, v):
        if know[e].get(sem, 0) >= v:
            return
        queue[e].wait_ge(T.sem[sem], v)
        know[e][sem] = v
        for s, w in clock.get((sem, v), {}).items():
            if know[e].get(s, 0) < w:
                know[e][s] = w

    def issue(e, fn, outs, ins, sem=None, inc=1):
        wr, rd = regs(outs), regs(ins)
        deps = set()
        for (rs, mine) in ((wr, True), (rd, False)):
            for (n2, a, b) in rs:
                for (lo, hi, w, eq, k) in log.get(n2, ()):
                    if a < hi and lo < b and (w or mine or (n2 in PSUM and eq != e)):
                        deps.add(k)
        for (rs, mine) in ((wr, True), (rd, False)):
            for (n2, a, b) in rs:
                log.setdefault(n2, []).append((a, b, mine, e, len(ops)))
        ops.append((e, fn, wr, rd, sem or "q" + e, inc, deps))

    def arrive(sem, v, outs):
        for (n2, a, b) in regs(outs):
            log.setdefault(n2, []).append((a, b, True, "r", len(ops)))
        ops.append(("r", None, regs(outs), [], sem, v, {len(ops) - 1}))

    def emit():
        order = ORDER if len(ORDER) == len(ops) else range(len(ops))
        done = {}
        for k in order:
            e, fn, _, _, sem, inc, deps = ops[k]
            count[sem] = count.get(sem, 0) + inc
            if e != "r":
                need = {}
                for j in deps:
                    need[done[j][0]] = max(need.get(done[j][0], 0), done[j][1])
                for s in sorted(need, key=lambda s: -len(clock.get((s, need[s]), {}))):
                    wait(e, s, need[s])
                ins_ = fn()
                if ins_ is not None:
                    ins_.then_inc(T.sem[sem], inc)
                clock[(sem, count[sem])] = dict(know[e])
            done[k] = (sem, count[sem])
        for sem in sorted(count):
            wait("y" if sem == "stored" else "g", sem, count[sem])

    def copy(out, in_):
        issue("v", lambda: g.vector.tensor_copy(out[0], in_[0]), [out], [in_])

    def tt(out, a, b, op):
        issue("v", lambda: g.vector.tensor_tensor(out[0], a[0], b[0], op), [out], [a, b])

    def ts(out, a, s1, op0, s2=None, op1=None):
        if op1 is None:
            issue("v", lambda: g.vector.tensor_scalar(out[0], a[0], val(s1), None, op0), [out], [a, s1])
        else:
            issue("v", lambda: g.vector.tensor_scalar(out[0], a[0], val(s1), val(s2), op0, op1), [out], [a, s1, s2])

    def scan(out, a, b, init, op0, op1):
        issue("v", lambda: g.vector.tensor_tensor_scan(out[0], a[0], b[0], val(init), op0, op1), [out], [a, b, init])

    def act(out, a, fn=Fn.Identity, bias=0.0, scale=1.0, acc=None):
        if acc is None:
            issue("s", lambda: g.scalar.activation(out[0], a[0], fn, bias=val(bias), scale=val(scale)), [out], [a, bias, scale])
        else:
            issue("s", lambda: g.scalar.activation(out[0], a[0], fn, bias=val(bias), scale=val(scale), accum_out=acc[0]),
                  [out, acc], [a, bias, scale])

    def iota(out, pat, base, mult, fl=False):
        if fl:
            issue("g", lambda: g.iota(out[0], pat, base, mult, allow_small_or_imprecise_dtypes=True), [out], [])
        else:
            issue("g", lambda: g.iota(out[0], pat, base, mult), [out], [])

    def mm(out, pairs):
        def fn():
            for k, (l, r) in enumerate(pairs):
                last = g.tensor.matmul(out[0], l[0], r[0], k == 0, k == len(pairs) - 1)
            return last
        issue("p", fn, [out], [x for p in pairs for x in p])

    def fold16(out, w, src, lo, n):
        mm(out, [(c(w, 15 - r, 143 - r), c(src, lo + r, lo + n, 16)) for r in range(16)])

    nld = [0]

    def load(e, out, src):
        sem = "ld%d" % nld[0]
        nld[0] += 1
        issue(e, lambda: queue[e].dma_start(out[0], src), [out], [], sem, 16)

    def store(dst, src):
        issue("y", lambda: g.sync.dma_start(dst, src[0]), [], [src], "stored", 16)

    nar = [0]

    def send(src, dst):
        sem = "ar%d" % nar[0]
        nar[0] += 1
        to = T.cores[(q + 1) % N]
        rid, pid, _ = topo.addr(to)

        def fn():
            g.remote_dma(dst[0], src[0], T.sem[sem], T.sem.sent, pid, rid, topo.mask(core, to))
        issue("g", fn, [], [src], "sent", len(topo.engines(core, to)))
        arrive(sem, len(topo.engines(T.cores[(q - 1) % N], core)), [dst])

    def common(a):
        m = -1
        for b in T.cores:
            if b != a:
                m &= topo.mask(a, b)
        return m

    def send_aims(r):
        o = 48 * r
        src = c("AL", o + 4 * (q // 2), o + 4 * (q // 2) + 4)
        slots = [c("AL", o + 12 + 4 * k, o + 16 + 4 * k) for k in range(1, N)]
        m = common(core)
        sem = "aim%ds" % r

        def fn():
            ids = [DstId(rid=topo.addr(b)[0], pnc=topo.addr(b)[1]) for b in others]
            g.remote_dma_fused([RemoteDMATransfer(dst_ids=ids, dma_engine_mask=m, remote_sem=T.sem[sem],
                                                  srcs=[src[0]], dsts=[s[0] for s in slots])], local_sem=T.sem.sent)
        issue("g", fn, [], [src], "sent", bin(m).count("1"))
        arrive(sem, sum(bin(common(b)).count("1") for b in others), slots)

    load("s", c("MI", 0, 60), T.mg[:])
    load("s", c("DI", 0, 96), T.dam[:, 0:96])
    load("s", c("AI", 0, 1), T.aim0[:])
    lc = _cuts(LOAD)
    load("y", c("SI", 0, 288), T.sire[:])
    for a, b in lc:
        load("y", c("TI", a, b), T.trait[:, a:b])
    load("y", c("DI", 96, 416), T.dam[:, 96:416])
    s1, s2 = ST[1], ST[2]
    iota(c("PI", 0, 1), [[0, 1]], 0, 1)
    iota(c("AR", 0, 16), [[1, 16]], 0, 0, True)
    iota(c("BASE", 0, 48), [[96, 4], [0, 12]], 0, 0)
    iota(c("X", s2 - E, s2), [[0, E]], 0, 0, True)
    iota(c("ID", 0, 160), [[-1, 160]], 16, 1, True)
    iota(c("X", F, s1), [[0, E]], 0, 0, True)
    iota(c("WB", 0, 144), [[0, 144]], 0, 0, True)
    ts(c("PJ", 0, 1), c("PI", 0, 1), 15, Op.bitwise_and)
    ts(c("PJ", 1, 2), c("PI", 0, 1), 4, Op.arith_shift_right)
    copy(c("PF", 0, 2), c("PJ", 0, 2))
    pm, gk = c("PF", 0, 1), c("PF", 1, 2)
    ts(c("I16", 0, 16), c("AR", 0, 16), pm, Op.is_equal)
    ts(c("WB", 15, 144, 16), c("AR", 0, 9), gk, Op.is_equal)

    ts(c("LI", 0, 48), c("MI", 12, 60), 15, Op.bitwise_and)
    copy(c("LU", 0, 48), c("LI", 0, 48))
    ts(c("HI", 0, 48), c("MI", 12, 60), 4, Op.arith_shift_right)
    tt(c("HJ", 0, 48), c("HI", 0, 48), c("BASE", 0, 48), Op.add)
    copy(c("HU", 0, 48), c("HJ", 0, 48))
    act(c("MK", 0, E), ind(c("I16", 0, 16), c("LU", 0, 12)))
    act(c("MK", E, 768), ind(c("I16", 0, 16), c("LU", 12, 48)))
    tt(c("Z", 576, 768), ind(c("DI", 0, 96), c("HU", 0, 12)), c("MK", 0, E), Op.mult)
    copy(c("MU", 0, 12), c("MI", 0, 12))
    own, nown = c("CC", 0, 1), c("CC", 1, 2)
    t0, h0 = c("TC", 0, 1), c("TH", 0, 1)
    copy(t0, c("AI", 0, 1))
    act(h0, t0, Fn.Identity, 0.0, 0.5)
    tt(c("Z", 0, 576), ind(c("SI", 0, 288), c("HU", 0, 36)), c("MK", 0, 576), Op.mult)
    fold16(c("BA", 0, 48), "WB", "Z", 0, 768)
    act(own, c("I16", 2 * q, 2 * q + 1), Fn.Identity, c("I16", 2 * q + 1, 2 * q + 2))
    act(c("J4", 0, 160), c("ID", 0, 160), Fn.Abs)
    act(nown, own, Fn.Identity, 1.0, -1.0)
    act(c("DM", 0, 16), c("I16", 0, 16), Fn.Identity, 0.0, own)
    act(c("ID", 0, 160), c("J4", 0, 160), Fn.Relu, 1.0, -1.0)
    act(c("HP", 0, 128), c("J4", 16, 144), Fn.Relu, 0.5, -1.0)
    act(c("HN", 0, 128), c("HP", 0, 128), Fn.Identity, 0.0, -1.0)
    act(c("WD", 0, 144), c("WB", 0, 144), Fn.Identity, 0.0, c("I16", (2 * q + 2) % 16, (2 * q + 2) % 16 + 1))
    ma, mb = c("I16", (2 * q + 2) % 16, (2 * q + 2) % 16 + 1), c("I16", (2 * q + 3) % 16, (2 * q + 3) % 16 + 1)
    act(c("WF", 0, 144), c("WB", 0, 144))
    act(c("CC", 6, 7), ma, Fn.Identity, mb)
    act(c("CC", 7, 8), mb, Fn.Identity, ma, -1.0)
    act(c("WH", 0, 144), c("WB", 0, 144), Fn.Identity, 0.0, c("CC", 6, 7))
    for r, eps in enumerate((128.0, 256.0)):
        act(c("CC", 2 + r, 3 + r), pm, Fn.Identity, 0.0, 1.0 / (8 * eps))
    iota(c("EF", 0, 128), [[-1, 2], [-2, 64]], 0, 1, True)
    iota(c("UF", 0, 10), [[16, 10]], 23, 0, True)
    iota(c("RS", 0, 8), [[0, 8]], 0, 0, True)
    act(c("CC", 4, 5), pm, Fn.Identity, -1024.0, 128.0)
    act(c("EF", 0, 128), c("EF", 0, 128), Fn.Abs)
    act(c("EB", 0, 128), c("EF", 0, 128), Fn.Relu, 1.0, -1.0)
    ts(c("CC", 5, 6), c("CC", 4, 5), 4.0, Op.mult, c("CC", 4, 5), Op.min)
    ts(c("UO", 0, 10), c("UF", 0, 10), c("CC", 5, 6), Op.add, 1031.0, Op.min)

    def founders(k):
        a, b = lc[k]
        copy(c("X", a, b), c("TI", a, b))
        act(c("TA", a, b), c("X", a, b), Fn.Abs, t0, -1.0)
        if a < NV:
            act(c("X2", a, min(b, NV)), c("X", a, min(b, NV)), Fn.Identity, 0.0, 2.0)

    copy(c("SU", 0, 288), c("SI", 0, 288))
    founders(0)
    for a in range(0, A, 384):
        iota(c("IO", a, a + 384), [[1, 384]], a, 0)
    founders(1)
    copy(c("CL", 0, 48), c("BA", 0, 48))
    for k in range(2, len(lc) - 1):
        founders(k)
    copy(c("SE0", 0, E), ind(c("TI", 0, F), c("MU", 0, 12)))
    send(c("SE0", 0, E), c("GU", 0, E))
    founders(len(lc) - 1)

    xf, xg = c("X", 0, F), c("X", 0, s1)
    act(c("SE1", 0, E), ind(xf, c("CL", 0, 12)))
    send(c("SE1", 0, E), c("GP", 0, E))
    iota(c("SEG", 0, 512), [[0, 32], [-32767, 16]], 1, 0, True)
    n = P1[0]
    copy(c("X", s1, s1 + n), ind(xf, c("SU", 0, n // 16)))
    act(c("X", s1 + n, s1 + A), ind(xf, c("SU", n // 16, 96)))
    tt(c("Z", 768, 1344), ind(c("DI", 0, 416), c("HU", 12, 48)), c("MK", E, 768), Op.mult)
    fold16(c("BB", 12, 48), "WB", "Z", 768, 576)
    copy(c("DU", 0, 416), c("DI", 0, 416))
    copy(c("X", s2, s2 + X2V), ind(c("X", 0, s1 + A), c("SU", 96, 96 + X2V // 16)))
    act(c("X", s2 + X2V, s2 + A), ind(c("X", 0, s1 + A), c("SU", 96 + X2V // 16, 192)))

    def x3(k):
        a, b = ([0] + X3P)[k], X3P[k]
        (act if k else copy)(c("X3", a, b), ind(c("X", 0, s2 + A), c("SU", 192 + a // 16, 192 + b // 16)))

    act(c("AV", 0, A), c("X", s1, s1 + A), Fn.Abs, h0, -0.5)
    copy(c("X", F, s1), c("GU", 0, E))
    copy(c("SE1", E, 2 * E), ind(xg, c("CL", 36, 48)))
    send(c("SE1", E, 2 * E), c("GP", E, 2 * E))
    n, m = P1[1], (P1[1] + A) // 64 * 32
    copy(c("MD", n, m), ind(xg, c("DU", n // 16, m // 16)))
    act(c("MD", 0, n), ind(xg, c("DU", 0, n // 16)))
    copy(c("MD", m, A), ind(xg, c("DU", m // 16, 96)))
    act(c("TA", s1, s1 + m), c("MD", 0, m), Fn.Abs, h0, -0.5)
    act(c("TA", s1 + m, s1 + A), c("MD", m, A), Fn.Abs, h0, -0.5)
    copy(c("CL", 48, 84), c("BB", 12, 48))
    x3(0)
    tt(c("TA", s1, s1 + m), c("TA", s1, s1 + m), c("AV", 0, m), Op.add)
    act(c("TA", F, s1), c("X", F, s1), Fn.Abs, t0, -1.0)
    x3(1)
    act(c("GT", 0, 2 * E), c("GP", 0, 2 * E), Fn.Abs, h0, -0.5)
    tt(c("TA", s1 + m, s1 + A), c("TA", s1 + m, s1 + A), c("AV", m, A), Op.add)
    hp, hn = c("HP", 0, 128), c("HN", 0, 128)
    for name, w, n in (("DL", hn, A), ("AV", hp, NP)):
        for a in range(0, n, 512):
            mm(c(name, a, a + 512), [(hp, c("X", s1 + a, s1 + a + 512)), (w, c("MD", a, a + 512))])

    def ghosts1(tb):
        tt(c(tb, s1 + A, s2), c("GT", 0, E), c("GT", E, 2 * E), Op.add)

    nse = [0]

    def sendbuf():
        nse[0] += 1
        return c("SE", E * (nse[0] - 1), E * nse[0])

    def least_tail(n, cut, r, win):
        big = c("R1", n - 1, n)
        act(c("JK", cut, n), c("R1", cut, n), Fn.Sign, big, -1.0, c("CN", 1, 2))
        ts(c("CN", 2, 3), c("R1", cut - 1, cut), big, Op.is_lt, float(cut), Op.mult)
        ts(c("IU", 0, 1), c("CN", 2, 3), c("CN", 0, 1), Op.max, c("CN", 1, 2), Op.add)
        tt(c("AL", 48 * r, 48 * r + 16), ind(win, c("IU", 0, 1)), c("DM", 0, 16), Op.mult)
        send_aims(r)

    def least_step(tb, s, a, b, cut):
        x = c(tb, s + a, s + b)
        scan(c("R1", a, b), x, x, 0.0 if a == 0 else c("R1", a - 1, a), Op.max, Op.max)
        if b == cut:
            act(c("JK", 0, cut), c("R1", 0, cut), Fn.Sign, c("R1", cut - 1, cut), -1.0, c("CN", 0, 1))

    def generation(tb, e, newest, pre=None):
        s = ST[e]
        ws, wd = c(tb, 0, s - E), c(tb, 0, s)
        cuts = _cuts(NEW if newest else GEN)
        o = (e - 1) * 96
        sb = sendbuf()
        sl, dl = c("CL", 12 * (e - 1), 12 * e), c("CL", 36 + 12 * (e - 1), 36 + 12 * e)
        copy(c("PE", 0, E), ind(ws, sl))
        if pre:
            pre()
        if newest:
            tt(sb, ind(wd, dl), c("PE", 0, E), Op.add)
        else:
            tt(c("QE", 0, E), ind(wd, dl), c("PE", 0, E), Op.add)
            ts(sb, c("QE", 0, E), 0.5, Op.mult)
        send(sb, c(tb, s + A, s + A + E))
        for a, b in cuts:
            act(c("AB", a, b), ind(ws, c("SU", o + a // 16, o + b // 16)))
        if newest:
            x3(2)
        cut = cuts[-1][0]
        for a, b in cuts:
            du = c("DU", o + a // 16, o + b // 16)
            if newest:
                tt(c(tb, s + a, s + b), ind(wd, du), c("AB", a, b), Op.add)
                if b >= cut:
                    least_step(tb, s, 0 if b == cut else a, b, cut)
            else:
                tt(c("AB", a, b), ind(wd, du), c("AB", a, b), Op.add)
                if b < A:
                    act(c(tb, s + a, s + b), c("AB", a, b), Fn.Identity, 0.0, 0.5)
                else:
                    ts(c(tb, s + a, s + b), c("AB", a, b), 0.5, Op.mult)
        return cut

    def sires_out(r):
        fold16(c("BB", 128, 192), ("WD", "WH")[r], ("PG", "PH")[r], 0, D)
        act(c("YS", 64 * r, 64 * r + 64), c("BB", 128, 192), Fn.Identity, float(ST[3 + r]))

    def choose(tb, r):
        e = 3 + r
        s, n = ST[e], (A if r == 0 else D)
        x = c(tb, s, s + n)
        ce = c("CC", 2 + r, 3 + r)
        scan(c("R2", 0, n), x, x, 1.0e9, Op.min, Op.min)
        o = 288 + 64 * r
        kv = KV[r]
        ts(c("K", 0, kv), ind(c(tb, 0, ST[e + 1]), c("DU", o, o + kv // 16)), -0.125, Op.mult, ce, Op.add)
        act(c("K", kv, D), ind(c(tb, 0, ST[e + 1]), c("DU", o + kv // 16, o + 64)), Fn.Identity, ce, -0.125)
        act(c("YF", 0, n), c("R2", 0, n), Fn.Sign, c("R2", n - 1, n), -1.0, c("CN", 4, 5))
        if r == 0:
            for a in range(0, A, 512):
                act(c("DL", a, a + 512), c("DL", a, a + 512), Fn.Abs)
            tt(c("MD", NP, A), c("MD", NP, A), c("X", s1 + NP, s1 + A), Op.add)
        ts(c("IU", 2 + 2 * r, 3 + 2 * r), c("CN", 4, 5), -1.0, Op.mult)

    def rows(r):
        bu = c("IU", 2 + 2 * r, 3 + 2 * r)
        for h, bank in enumerate(("BA", "BB")):
            def fn(h=h, bank=bank):
                for u in range(4):
                    last = g.tensor.transpose(c(bank, 128 * u, 128 * u + 128)[0], T.K[:, 4 * h + u:D:8], T.ID[:, 16:144])
                return last
            issue("p", fn, [c(bank, 0, 512)], [c("K", 0, D), c("ID", 0, 160)])
            scan(c("RS", 8 + 512 * h, 520 + 512 * h), c("SEG", 0, 512), c(bank, 0, 512), 0.0, Op.max, Op.min)
        act(c("UB", 0, 144), ind(c("RS", 0, 1032), c("UO", 0, 9)), Fn.Identity, 0.0, 1024.0 * (r + 1))
        mm(c("BB", 0, 64), [(c("UB", 8, 136), c("EB", 0, 64)), (c("UB", 0, 128), c("EB", 64, 128))])
        ml = c("MM", 64 * r, 64 * r + 64)
        if r == 0:
            ts(c("P16", 48, 64), ind(c("IO", 0, A), bu), nown, Op.mult)
            act(c("P16", 64, 80), ind(c("X3", 0, A), bu), Fn.Identity, 0.0, own)
            tt(c("P16", 0, 16), c("P16", 48, 64), c("P16", 64, 80), Op.add)
        else:
            copy(c("P16", 16, 32), ind(c("IO", 0, A), bu))
            act(c("PB", 0, 16), c("P16", 16, 32))
            act(c("P16", 48, 64), c("P16", 16, 32), Fn.Identity, 0.0, mb)
            act(c("P16", 64, 80), c("PB", 0, 16), Fn.Identity, 0.0, c("CC", 7, 8))
            tt(c("P16", 32, 48), c("P16", 48, 64), c("P16", 64, 80), Op.add)
        copy(c("UJ", 0, 64), c("BB", 0, 64))
        ts(c("DI", 288, 352), c("UJ", 0, 64), 15, Op.bitwise_and)
        copy(ml, c("DI", 288, 352))
        if r == 0:
            tt(c("ZM", 0, E), ind(c("DI", 0, 352), c("HU", 36, 48)), c("MK", 576, 768), Op.mult)
            fold16(c("BB", 64, 76), "WF", "ZM", 0, E)

    def payload(r, part):
        pg, p16, n = ("PG" if r == 0 else "PH"), c("P16", 32 * r, 32 * r + 16), PVR[r]
        if part == 0:
            copy(c(pg, 0, n), ind(p16, c("MM", 64 * r, 64 * r + n // 16)))
        else:
            act(c(pg, n, D), ind(p16, c("MM", 64 * r + n // 16, 64 * r + 64)))

    def start_round(tb, r):
        t, h, tv = c("TC", r, r + 1), c("TH", r, r + 1), c("TV", r, r + 1)
        al = c("AL", 48 * (r - 1), 48 * (r - 1) + 44)
        act(c("J3", 48 * (r - 1), 48 * (r - 1) + 44), al, Fn.Identity, 0.0, 1.0, t)
        issue("v", lambda: g.vector.tensor_reduce(tv[0], al[0], Ax.X, Op.add), [tv], [al])
        act(c(tb, s1, s1 + NP), c("AV", 0, NP), Fn.Abs, t, -1.0)
        act(h, t, Fn.Identity, 0.0, 0.5)
        act(c(tb, s1 + NP, s1 + A), c("MD", NP, A), Fn.Abs, t, -0.5)
        for a in range(0, NV, 512):
            ts(c("BA", 0, 512), c("X2", a, a + 512), tv, Op.subtract, tv, Op.max)
            tt(c(tb, a, a + 512), c("BA", 0, 512), c("X", a, a + 512), Op.subtract)
        act(c("GT", 0, 2 * E), c("GP", 0, 2 * E), Fn.Abs, h, -0.5)
        act(c(tb, NV, s1), c("X", NV, s1), Fn.Abs, t, -1.0)
        tt(c(tb, s1, s1 + A), c(tb, s1, s1 + A), c("DL", 0, A), Op.max)
        ghosts1(tb)
        if r == 1:
            copy(c("CM", 0, 12), c("BB", 64, 76))

    def fourth(tb, r):
        s = ST[4]
        wd = c(tb, 0, s)
        if r == 1:
            payload(0, 0)
        t16 = c("T16", 16 * r, 16 * r + 16)
        ts(t16, ind(c(tb, ST[3], ST[3] + A), c("IU", 2, 3)), 0.5, Op.mult)
        act(c("QE", 0, E), ind(wd, c("CL", 72, 84)), Fn.Identity, 0.0, 0.5)
        sb = sendbuf()
        cuts = _cuts(G4)
        ts(c("AB", 0, G4V), ind(wd, c("DU", 288, 288 + G4V // 16)), 0.5, Op.mult)
        tt(sb, ind(t16, c("CM", 0, 12)), c("QE", 0, E), Op.add)
        send(sb, c(tb, s + D, s + D + E))
        cut = cuts[-1][0]
        for k, (a, b) in enumerate(cuts):
            lo = G4V if k == 0 else a
            act(c("AB", lo, b), ind(wd, c("DU", 288 + lo // 16, 288 + b // 16)), Fn.Identity, 0.0, 0.5)
        if r == 1:
            payload(0, 1)
        for k, (a, b) in enumerate(cuts):
            tt(c(tb, s + a, s + b), ind(t16, c("MM", a // 16, b // 16)), c("AB", a, b), Op.add)
            if r == 1 and b >= cut:
                least_step(tb, s, 0 if b == cut else a, b, cut)
            if r == 2:
                act(c("YF", a, b), c(tb, s + a, s + b), Fn.Identity, 65535.0, -1.0)
                store(T.yf[:, a:b], c("YF", a, b))
        return cut

    generation("TA", 2, False, lambda: ghosts1("TA"))
    cut = generation("TA", 3, True)
    least_tail(A, cut, 0, c("X3", 0, A))
    choose("TA", 0)
    rows(0)
    start_round("TB", 1)
    generation("TB", 2, False)
    generation("TB", 3, False)
    cut = fourth("TB", 1)
    least_tail(D, cut, 1, c("PG", 0, D))
    choose("TB", 1)
    rows(1)
    start_round("TA", 2)
    store(T.yt[:], c("TC", 1, 3))
    generation("TA", 2, False)
    sires_out(0)
    generation("TA", 3, False)
    fourth("TA", 2)
    t16 = c("T16", 48, 64)
    ts(t16, ind(c("TA", ST[4], ST[4] + D), c("IU", 4, 5)), -0.5, Op.mult)
    payload(1, 0)
    payload(1, 1)
    wd = c("TA", 0, ST[5])
    cuts = _cuts(G5)
    for k, (a, b) in enumerate(cuts):
        if k == 0:
            ts(c("AB", a, G5V), ind(wd, c("DU", 352 + a // 16, 352 + G5V // 16)), -0.5, Op.mult, 65535.0, Op.add)
            a = G5V
        act(c("AB", a, b), ind(wd, c("DU", 352 + a // 16, 352 + b // 16)), Fn.Identity, 65535.0, -0.5)
    for k, (a, b) in enumerate(cuts):
        tt(c("YF", D + a, D + b), ind(t16, c("MM", 64 + a // 16, 64 + b // 16)), c("AB", a, b), Op.add)
        store(T.yf[:, D + a:D + b], c("YF", D + a, D + b))
        if k == 0:
            sires_out(1)
            store(T.ys[:], c("YS", 0, 128))
    emit()
